import numpy as np, ml_dtypes
CORES = [3,7,11,15,131,135,139,143]
N = 8
BF = ml_dtypes.bfloat16
def gentries(a):
    return np.ascontiguousarray(a.reshape(8, 16, -1).transpose(0, 2, 1)).reshape(8, -1)
def gtable(e):
    e = np.asarray(e); return np.ascontiguousarray(e.reshape(8, -1, 16).transpose(0, 2, 1)).reshape(128, -1).astype(np.int32)
def f(rng, *shape):
    return (rng.standard_normal(shape, dtype=np.float32) * np.exp2(rng.integers(-2, 3, shape[:-1] + (1,)))).astype(BF)
def wide(rng, *shape):
    v = f(rng, *shape).astype(np.float32); k = shape[:-2] + (1, shape[-1])
    return (v * np.exp2(rng.integers(-6, 7, k)) * (rng.random(k) > 0.0625)).astype(BF)
M, A, L, C, SR, SA = 2048, 512, 3, 4, 128, 64
def first(l):
    return M + N * SR + (l - 1) * (A + N * SA)
def glists(e):
    return np.stack([gtable(e[r].reshape(8, -1)) for r in range(N)])
def grow(rng, n):
    v = rng.standard_exponential((N, 8, 16, n), dtype=np.float32) * (rng.random((N, 8, 16, n)) < 0.75) * (0.5 + rng.random((N, 8, 1, n)))
    return np.add.accumulate(v, axis=2).reshape(N, 128, n).astype(BF)
def draw_parts(rng):
    e = np.zeros((N, 8, L, 2 * C, A), np.int64); k = (N, 8, 2 * C, A)
    for l in range(1, L + 1):
        e[:, :, l - 1] = rng.integers(0, first(l), k)
        if l > 1: e[:, :, l - 1] = np.where(rng.random(k) < 0.5, rng.integers(first(l - 1), first(l), k), e[:, :, l - 1])
    return e
def draw(rng, e):
    return {"sup": grow(rng, M), "cap": grow(rng, L * A), "stock": (8 * rng.random((N, 128, L * A)) * (rng.random((N, 128, L * A)) < 0.8)).astype(BF), "parts": glists(e),
            "ship": glists(rng.integers(0, M, (N, 8, N * SR))), "hand": glists(rng.integers(0, A, (N, 8, (L - 1) * N * SA)))}
def setup_inputs(rng):
    return draw(rng, draw_parts(rng))
def setup_inputs_ties(rng):
    e = draw_parts(rng); e[:, :, :, 1:C] = np.where(rng.random((N, 8, L, C - 1, A)) < 0.3, e[:, :, :, :1], e[:, :, :, 1:C])
    e[:, :, :, C:] = np.where(rng.random((N, 8, L, C, A)) < 0.2, e[:, :, :, :C], e[:, :, :, C:])
    d = draw(rng, e)
    d["sup"] = np.add.accumulate(rng.integers(0, 2, (N, 8, 16, M)), axis=2).reshape(N, 128, M).astype(np.float32).astype(BF)
    d["cap"] = np.add.accumulate(rng.integers(0, 3, (N, 8, 16, L * A)), axis=2).reshape(N, 128, L * A).astype(np.float32).astype(BF)
    d["stock"] = rng.integers(0, 4, (N, 128, L * A)).astype(np.float32).astype(BF); return d
def setup_inputs_ends(rng):
    e = draw_parts(rng)
    for l in range(1, L + 1):
        b = [0, M - 1, M, M + N * SR - 1]
        for m in range(1, l): b += [first(m), first(m) + A - 1, first(m) + A, first(m + 1) - 1]
        k = (N, 8, 2 * C, A); e[:, :, l - 1] = np.where(rng.random(k) < 0.5, rng.choice(np.array(b), k), e[:, :, l - 1])
        for r in range(N):
            q = (r + 1) % N
            for g in range(8):
                if l == 1: e[r, g, 0, 0, :SR] = M + q * SR + rng.permutation(SR)
                else: e[r, g, l - 1, 0, :SA] = first(l - 1) + A + q * SA + rng.permutation(SA)
    d = draw(rng, e)
    s = rng.integers(0, M, (N, 8, N, SR)); s[..., 0] = 0; s[..., -1] = M - 1; d["ship"] = glists(s)
    h = rng.integers(0, A, (N, 8, L - 1, N, SA)); h[..., 0] = A - 1; h[..., -1] = 0; d["hand"] = glists(h); return d
def setup_inputs_one(rng):
    e = np.zeros((N, 8, L, 2 * C, A), np.int64); a = rng.integers(1, N); k = (8, 2 * C, A)
    for r in range(N):
        q = (r + a) % N; e[r, :, 0] = M + q * SR + rng.integers(0, SR, k)
        for l in range(2, L + 1): e[r, :, l - 1] = first(l - 1) + A + q * SA + rng.integers(0, SA, k)
    d = draw(rng, e); s = rng.integers(0, M, (N, 8, N, SR)); q = rng.integers(0, N); s[q] = s[q][..., :1]; d["ship"] = glists(s); return d
def setup_inputs_late(rng):
    d = setup_inputs(rng); v = d["sup"].astype(np.float32).reshape(N, 8, 16, M); v[:, :, 15] = 64 - v[:, :, 14]; d["sup"] = v.reshape(N, 128, M).astype(BF)
    c = d["cap"].astype(np.float32).reshape(N, 8, 16, L * A); t = rng.integers(0, 14, (N, 8, 1, L * A))
    d["cap"] = np.where(np.arange(16)[:, None] < t - 4, np.float32(0), 8 * c).reshape(N, 128, L * A).astype(BF); return d
def setup_inputs_spread(rng):
    d = setup_inputs(rng)
    for k, n in (("sup", M), ("cap", L * A), ("stock", L * A)): d[k] = (wide(rng, N, 128, n).astype(np.float32) * np.float32(2.0 ** 40)).astype(BF)
    return d
def check_inputs(d):
    bad = []
    try:
        for k in ("sup", "cap", "stock"):
            v = d[k].astype(np.float32)
            if not (np.isfinite(v).all() and (np.abs(v) <= 2.0 ** 60).all()): bad.append(k)
        e = np.stack([gentries(v) for v in d["parts"]]).reshape(N, 8, L, 2 * C * A)
        if any((e[:, :, l - 1] < 0).any() or (e[:, :, l - 1] >= first(l)).any() for l in range(1, L + 1)): bad.append("parts")
        for k, n in (("ship", M), ("hand", A)):
            if (d[k] < 0).any() or (d[k] >= n).any(): bad.append(k)
    except Exception:
        bad.append("shapes")
    return bad
def reference(sup, cap, stock, parts, ship, hand):
    raw = sup.astype(np.float32).reshape(N, 8, 16, M); ca = cap.astype(np.float32).reshape(N, 8, 16, L, A); st = stock.astype(np.float32).reshape(N, 8, 16, L, A)
    e = [gentries(v).reshape(8, L, 1, 2 * C * A) for v in parts]; sh = [gentries(v).reshape(8, 1, N, SR) for v in ship]; ha = [gentries(v).reshape(8, 1, L - 1, N, SA) for v in hand]
    w = np.zeros((N, 8, 16, first(L)), np.float32); now = np.zeros((N, 8, 16, A), np.float32)
    w[..., :M] = raw; h = A // 2
    for r in range(N):
        for q in range(N): w[r, :, :, M + q * SR:M + (q + 1) * SR] = np.take_along_axis(raw[q], sh[q][:, :, r], 2)
    for l in range(1, L + 1):
        for r in range(N):
            v = np.take_along_axis(w[r], e[r][:, l - 1], 2).reshape(8, 16, 2 * C, A)
            i = np.argmin(v[:, 15, :C], axis=1)
            hit = np.arange(C)[:, None] == i[:, None]
            z = np.min(np.where(hit[:, None], v[:, :, C:], v[:, :, :C]), axis=2)
            s = np.zeros_like(z); s[:, 1:, :h] = z[:, :-1, :h]; s[:, 2:, h:] = z[:, :-2, h:]
            now[r] = np.minimum(s, ca[r, :, :, l - 1]) + st[r, :, :, l - 1]
        if l < L:
            b = first(l); w[:, :, :, b:b + A] = now
            for r in range(N):
                for q in range(N): w[r, :, :, b + A + q * SA:b + A + (q + 1) * SA] = np.take_along_axis(now[q], ha[q][:, :, l - 1, r], 2)
    return {"y": now.reshape(N, 128, A)}

@@ -1,0 +1,316 @@
+import numpy as np
+from concourse.bass import DstId, RemoteDMATransfer
+from concourse.mybir import AluOpType as OP, ActivationFunctionType as AF
+
+M, A, L, SR, SA, N = 2048, 512, 3, 128, 64, 8
+H = A // 2
+PEN = 8192.0
+
+
+def first(l):
+    return M + N * SR + (l - 1) * (A + N * SA)
+
+
+BF, F32, I32, U16 = "bfloat16", "float32", "int32", "uint16"
+NV = 288
+SCRATCH = {
+    "WB": ("sbuf", [128, M + N * SR], BF),
+    "W": ("sbuf", [128, first(L)], F32),
+    "shipi": ("sbuf", [128, 64], I32), "handi": ("sbuf", [128, 64], I32),
+    "ship16": ("sbuf", [128, 64], U16), "hand16": ("sbuf", [128, 64], U16),
+    "PT": ("sbuf", [128, 768], I32), "cu": ("sbuf", [128, 384], U16),
+    "CF": ("sbuf", [128, 128], F32), "TL": ("sbuf", [128, 128], F32), "VB": ("sbuf", [128, L * NV], F32),
+    "SB": ("sbuf", [128, N * SR], BF), "SH1": ("sbuf", [128, N * SA], F32), "SH2": ("sbuf", [128, N * SA], F32),
+    "GB": ("sbuf", [128, 2 * A], BF), "MB": ("sbuf", [128, 2 * A], BF), "GF": ("sbuf", [128, 2 * A], F32), "MF": ("sbuf", [128, 2 * A], F32),
+    "E": ("sbuf", [128, 192], F32), "BT": ("sbuf", [128, 192], BF), "HT": ("sbuf", [128, 192], BF),
+    "SC": ("sbuf", [128, 256], F32), "RS": ("sbuf", [128, 256], F32), "sel": ("sbuf", [128, 96], U16),
+    "XB0": ("sbuf", [128, A], BF), "XB1": ("sbuf", [128, A], BF), "XF0": ("sbuf", [128, A], F32), "XF1": ("sbuf", [128, A], F32),
+    "C1": ("sbuf", [128, L * A], BF), "C2": ("sbuf", [128, L * A], BF), "MC": ("sbuf", [128, L * A], BF), "ST": ("sbuf", [128, L * A], BF),
+    "YB": ("sbuf", [128, A], F32),
+    "dist": ("sbuf", [128, 128], I32), "dm": ("sbuf", [128, 128], I32), "dmb": ("sbuf", [128, 128], I32), "m16": ("sbuf", [128, 128], I32),
+    "bit4": ("sbuf", [128, 128], I32), "dp": ("sbuf", [128, 128], I32), "dq": ("sbuf", [128, 32], I32), "pos": ("sbuf", [128, 32], I32), "posm": ("sbuf", [128, 32], I32),
+    "a1": ("sbuf", [128, 128], BF), "a2": ("sbuf", [128, 128], BF), "k1": ("sbuf", [128, 128], BF), "k2": ("sbuf", [128, 128], BF),
+    "sb1": ("sbuf", [128, 128], BF), "sb2": ("sbuf", [128, 128], BF), "sf1": ("sbuf", [128, 128], F32), "sf2": ("sbuf", [128, 128], F32),
+    "e1": ("sbuf", [128, 128], BF), "e2": ("sbuf", [128, 128], BF), "idn": ("sbuf", [128, 128], BF), "idf": ("sbuf", [128, 128], F32),
+    "x00": ("sbuf", [128, 128], F32), "x01": ("sbuf", [128, 128], F32), "x10": ("sbuf", [128, 128], F32), "x11": ("sbuf", [128, 128], F32),
+    "pmp": ("sbuf", [128, 128], BF), "pmn": ("sbuf", [128, 128], BF), "pm5": ("sbuf", [128, 128], BF),
+    "qb": ("sbuf", [128, 32], BF), "qf": ("sbuf", [128, 32], F32),
+    "PA": ("psum", [128, 512], F32), "PB": ("psum", [128, 512], F32), "PH": ("psum", [128, 512], F32), "PL": ("psum", [128, 512], F32),
+    "P0": ("psum", [128, 512], F32), "P1": ("psum", [128, 512], F32), "P2": ("psum", [128, 512], F32),
+}
+NPOOL = 140
+SEMAPHORES = ["arr0", "arr1", "arr2", "loc0", "loc1", "loc2"] + ["s%d" % i for i in range(NPOOL)]
+PIECES = [(0, 256, 1), (256, 384, 2), (384, 512, 2)]
+ON_S = [(0, 0, 128), (0, 128, 256), (0, 256, 512), (1, 0, 256), (1, 256, 512)]
+ON_V = [(0, 0, 128), (0, 128, 256), (0, 256, 512), (1, 0, 256), (1, 256, 384), (1, 384, 512)]
+BLOCKS = [("G", 0, 0), ("M", 0, 0), ("G", 0, 1), ("M", 0, 1), ("G", 0, 2), ("G", 0, 3), ("M", 0, 2), ("M", 0, 3),
+          ("G", 1, 0), ("G", 1, 1), ("G", 1, 2), ("G", 1, 3), ("M", 1, 0), ("M", 1, 1), ("M", 1, 2), ("M", 1, 3)]
+
+
+def rank_program(g, core, T, topo):
+    rank = T.rank_of(core)
+    if rank is None:
+        return
+    Q = {"v": g.vector, "s": g.scalar, "t": g.tensor, "g": g, "y": g.sync}
+    pool, total, seen, best = {}, {}, {q: {} for q in Q}, {}
+
+    def wait(q, tok):
+        name, val = tok
+        if seen[q].get(name, 0) >= val:
+            return
+        Q[q].wait_ge(T.sem[name], val)
+        seen[q][name] = val
+        best[name] = max(best.get(name, 0), val)
+
+    def do(q, fn, role, deps, n=1):
+        for d in deps:
+            wait(q, d)
+        inst = fn()
+        if role is None:
+            return None
+        if role not in pool:
+            pool[role] = "s%d" % len(pool)
+        name = pool[role]
+        inst.then_inc(T.sem[name], n)
+        total[name] = total.get(name, 0) + n
+        return (name, total[name])
+
+    V, S, PE = g.vector, g.scalar, g.tensor
+
+    def tt(out, a, b, op, role, deps):
+        return do("v", lambda: V.tensor_tensor(out=out, in0=a, in1=b, op=op), role, deps)
+
+    def ts(out, a, s1, op, role, deps):
+        return do("v", lambda: V.tensor_scalar(out=out, in0=a, scalar1=s1, scalar2=None, op0=op), role, deps)
+
+    def vcopy(out, a, role, deps):
+        return do("v", lambda: V.tensor_copy(out=out, in_=a), role, deps)
+
+    def scopy(out, a, role, deps):
+        return do("s", lambda: S.activation(out=out, in_=a, func=AF.Copy), role, deps)
+
+    def mm(out, w, m, start, stop, role, deps):
+        return do("t", lambda: PE.matmul(out=out, lhsT=w, rhs=m, start=start, stop=stop), role, deps)
+
+    def dma(q, out, in_, role, deps=()):
+        return do(q, lambda: Q[q].dma_start(out=out, in_=in_), role, deps, 16)
+
+    def iota(out, pat, base, cm, role):
+        return do("g", lambda: g.iota(out, pat, base, cm), role, [])
+
+    here = topo.cores_of(core)
+    far = [r for r in range(N) if topo.host(T.cores[r]) != topo.host(core)]
+    buddy = [r for r in range(N) if T.cores[r] in here and r != rank]
+    near = [r for r in range(N) if r not in far and r not in buddy and r != rank]
+    off = topo.engines(core, T.cores[far[0]])
+    rest = [e for e in topo.engines(core, T.cores[buddy[0]]) if e not in off]
+    share = {}
+    for grp in (far, near):
+        k = len(off) // len(grp)
+        for j, r in enumerate(grp):
+            share[r] = off[j * k:(j + 1) * k]
+    for j, r in enumerate(buddy):
+        share[r] = rest[4 * j:4 * j + 4:2]
+    landed = sum(len(v) for v in share.values())
+
+    def send(ranks, src, dst, w_src, w_dst, k, deps):
+        for d in deps:
+            wait("g", d)
+        tr = []
+        for r in ranks:
+            rid, pid = topo.addr(T.cores[r], core)
+            tr.append(RemoteDMATransfer(src=src[:, r * w_src:(r + 1) * w_src], dst=dst[:, w_dst + rank * w_src:w_dst + (rank + 1) * w_src],
+                                        dst_ids=[DstId(rid=rid, pnc=pid)], dma_engine_mask=sum(1 << e for e in share[r]),
+                                        remote_sem=T.sem["arr%d" % k]))
+        g.remote_dma_fused(tr, local_sem=T.sem["loc%d" % k])
+
+    def runs(ranks):
+        out = []
+        for r in ranks:
+            if out and out[-1][1] == r:
+                out[-1][1] = r + 1
+            else:
+                out.append([r, r + 1])
+        return out
+
+    def hand_over(win, lists, col0, per, stage, dst, w_dst, k, deps):
+        per16 = per // 16
+
+        def pick(q, ranks, tag):
+            got = []
+            for j, (b, e) in enumerate(runs(ranks)):
+                o, i = stage[:, b * per:e * per], win.indirect(lists[:, col0 + b * per16:col0 + e * per16])
+                got.append((vcopy if q == "v" else scopy)(o, i, "hand%s%s%d" % (q, tag, j), deps))
+            return got
+        h = len(far) // 2
+        t1 = pick("v", far[:h], "f") + pick("s", far[h:], "f")
+        t2 = pick("v", near, "n") + pick("s", buddy, "b")
+        own = scopy(dst[:, w_dst + rank * per:w_dst + (rank + 1) * per], win.indirect(lists[:, col0 + rank * per16:col0 + (rank + 1) * per16]), "handown", deps)
+        send(far, stage, dst, per, w_dst, k, t1)
+        send(near + buddy, stage, dst, per, w_dst, k, t2)
+        return own
+
+    t_sup = dma("y", T.WB[:, 0:M], T.sup[:], "sup")
+    t_ship = dma("s", T.shipi[:], T.ship[:], "ship")
+    t_pt = {1: dma("s", T.PT[:, 0:256], T.parts[:, 0:256], "pt1")}
+    t_hand = dma("s", T.handi[:], T.hand[:], "hand")
+
+    t_dist = iota(T.dist[:], [[1, 128]], 128, -1, "dist")
+    t_bit = iota(T.bit4[:], [[0, 4], [128, 2], [0, 16]], 0, 0, "bit4")
+    t_dp = iota(T.dp[:], [[-4, 8], [-1, 4], [-32, 4]], 0, 1, "dp")
+    t_dq = iota(T.dq[:], [[0, 4], [-16, 8]], -15, 1, "dq")
+    t_m16 = iota(T.m16[:], [[0, 8], [1, 16]], 0, 0, "m16")
+    t_pos = iota(T.pos[:], [[1, 32]], 0, 32, "pos")
+    t_r0 = do("v", lambda: V.memset(T.RS[:], 0.0), "rs0", [])
+    t_rs = do("v", lambda: V.memset(T.RS[:, 0:256:4], -1048576.0), "rs", [t_r0])
+    t_dm = ts(T.dm[:], T.dist[:], 127, OP.bitwise_and, "dm", [t_dist])
+    t_dmb = tt(T.dmb[:], T.dm[:], T.bit4[:], OP.add, "dmb", [t_dm, t_bit])
+    t_x = [ts(T[n][:], T.dmb[:], v, OP.is_equal, n, [t_dmb]) for n, v in (("x00", 0), ("x11", 128), ("x01", 144), ("x10", 112))]
+    X = [[T.x00, T.x01], [T.x10, T.x11]]
+    t_idn = ts(T.idn[:], T.dm[:], 0, OP.is_equal, "idn", [t_dm])
+    t_pm = [do("v", lambda: V.tensor_scalar(out=T[n][:], in0=T.dp[:], scalar1=0, scalar2=v, op0=OP.is_equal, op1=OP.mult), n, [t_dp])
+            for n, v in (("pmp", PEN), ("pmn", -PEN), ("pm5", -512.0))]
+    t_qb = ts(T.qb[:], T.dq[:], 0, OP.is_equal, "qb", [t_dq])
+    t_s, t_e, t_sf = {}, {}, {}
+    for ld in (1, 2):
+        ta = ts(T["a%d" % ld][:], T.dm[:], ld, OP.is_equal, "a%d" % ld, [t_dm])
+        tk = ts(T["k%d" % ld][:], T.m16[:], ld, OP.is_ge, "k%d" % ld, [t_m16])
+        t_s[ld] = tt(T["sb%d" % ld][:], T["a%d" % ld][:], T["k%d" % ld][:], OP.mult, "sb%d" % ld, [ta, tk])
+        t_e[ld] = tt(T["e%d" % ld][:], T["a%d" % ld][:], T["sb%d" % ld][:], OP.subtract, "e%d" % ld, [t_s[ld]])
+    t_posm = ts(T.posm[:], T.pos[:], 511, OP.bitwise_and, "posm", [t_pos])
+    t_idf = scopy(T.idf[:], T.idn[:], "idf", [t_idn])
+    t_qf = scopy(T.qf[:], T.qb[:], "qf", [t_qb])
+
+    t_ship16 = vcopy(T.ship16[:], T.shipi[:], "ship16", [t_ship])
+    t_own = hand_over(T.WB[:, 0:M], T.ship16, 0, SR, T.SB, T.WB, M, 0, [t_ship16, t_sup])
+
+    wait("y", ("loc0", landed))
+    t_cap, t_st = {}, {}
+    wr = [dma("y", T.C1[127:128, :], T.cap[0:1, :], "capw1"), dma("y", T.C2[126:128, :], T.cap[0:2, :], "capw2")]
+
+    def load_cap(l):
+        b = (l - 1) * A
+        t_cap[l] = wr + [dma("y", T.C1[0:127, b:b + H], T.cap[1:128, b:b + H], "cap1_%d" % l),
+                         dma("y", T.C2[0:126, b + H:b + A], T.cap[2:128, b + H:b + A], "cap2_%d" % l)]
+    load_cap(1)
+    t_st[1] = dma("y", T.ST[:, 0:A], T.stock[:, 0:A], "st1")
+    t_pt[2] = t_pt[3] = dma("y", T.PT[:, 256:768], T.parts[:, 256:768], "pt2")
+    load_cap(2)
+    load_cap(3)
+    t_st[2] = t_st[3] = dma("y", T.ST[:, A:3 * A], T.stock[:, A:3 * A], "st2")
+
+    t_cu, t_pre, t_mc = {}, {}, {}
+
+    def prep_first(l):
+        b = (l - 1) * 256
+        t_cf = vcopy(T.CF[:], T.PT[:, b:b + 128], "CF", [t_pt[l]])
+        t_tl = do("v", lambda: V.transpose(out=T.TL[:], in_=T.CF[:]), "TL", [t_cf])
+        for i in range(4):
+            for hb in range(2):
+                for e in range(2):
+                    t_pl = mm(T.PL[:, i * 32 + hb:(i + 1) * 32:2], X[hb][e][:], T.TL[:, i * 32 + 16 * e:i * 32 + 16 * e + 16], e == 0, e == 1, "PL", t_x + [t_tl])
+        return t_pl
+
+    def prep_offsets(l, t_pl):
+        c = (l - 1) * 128
+        t_cu[l] = vcopy(T.cu[:, c:c + 128], T.PL[:, 0:128], "cu", [t_pl])
+
+    def prep_lists(l):
+        b, o = (l - 1) * 256, (l - 1) * NV
+        got = []
+        for i, pen in enumerate((0.0, -PEN, -PEN, -2 * PEN)):
+            for k, p in ((0, b + (i ^ 1) * 32), (1, b + 128 + i * 32)):
+                got.append(ts(T.VB[:, o + k * 128 + i:o + (k + 1) * 128:4], T.PT[:, p:p + 32], pen, OP.add, "vb%d%d" % (k, i), [t_pt[l]]))
+        got.append(ts(T.VB[:, o + 256:o + NV], T.posm[:], 512.0, OP.add, "vbm", [t_posm]))
+        t_pre[l] = mm(T.PH[:, 0:NV], T.idf[:], T.VB[:, o:o + NV], True, False, "pre", got + [t_idf])
+
+    def prep_cap(l):
+        b = (l - 1) * A
+        t_mc[l] = [ts(T.MC[:, b:b + H], T.C1[:, b:b + H], 0.0, OP.min, "mc1", t_cap[l]),
+                   ts(T.MC[:, b + H:b + A], T.C2[:, b + H:b + A], 0.0, OP.min, "mc2", t_cap[l])]
+
+    t_pl = prep_first(1)
+    prep_lists(1)
+    prep_offsets(1, t_pl)
+    t_hand16 = vcopy(T.hand16[:], T.handi[:], "hand16", [t_hand])
+    for ld in (1, 2):
+        t_sf[ld] = scopy(T["sf%d" % ld][:], T["sb%d" % ld][:], "sf%d" % ld, [t_s[ld]])
+    t_conv = [scopy(T.W[:, 0:M // 2], T.WB[:, 0:M // 2], "convs", [])]
+
+    ready = [t_own, t_sup, ("arr0", landed)]
+    t_ev = []
+    for l in range(1, L + 1):
+        raw = l == 1
+        win = (T.WB if raw else T.W)[:, 0:first(l)]
+        G, MN = (T.GB, T.MB) if raw else (T.GF, T.MF)
+        XX = (T.XB0, T.XB1) if raw else (T.XF0, T.XF1)
+        c = (l - 1) * 128
+        t_g, t_m = {}, {}
+        for p, a0, a1 in ON_S:
+            li = T.cu[:, c + 2 * p * 32 + a0 // 16:c + 2 * p * 32 + a1 // 16]
+            t_g[(p, a0, a1)] = scopy(G[:, p * A + a0:p * A + a1], win.indirect(li), "g%d_%d" % (p, a0), ready + [t_cu[l]])
+        for p, a0, a1 in ON_V:
+            li = T.cu[:, c + (2 * p + 1) * 32 + a0 // 16:c + (2 * p + 1) * 32 + a1 // 16]
+            t_m[(p, a0, a1)] = tt(MN[:, p * A + a0:p * A + a1], win.indirect(li), G[:, p * A + a0:p * A + a1], OP.min, "m%d_%d" % (p, a0),
+                                  ready + [t_cu[l]] + [t_g[k] for k in t_g if k[0] == p and k[1] < a1 and a0 < k[2]])
+        q = T.qb if raw else T.qf
+        for kind, p, y in BLOCKS:
+            toks, src = (t_g, G) if kind == "G" else (t_m, MN)
+            dep = [toks[k] for k in toks if k[0] == p and k[1] <= 128 * y < k[2]] + [t_qb if raw else t_qf]
+            w = src[:, p * A + 128 * y:p * A + 128 * y + 128]
+            if (kind, p) == ("M", 1):
+                t_pb = mm(T.PB[:, y:128:4], w, q[:, 0:32], True, True, "PB", dep)
+            else:
+                o = {("G", 1): 0, ("M", 0): 64, ("G", 0): 128}[(kind, p)]
+                t_pa = mm(T.PA[:, o + y:o + 64:4], w, q[:, 0:16], True, True, "PA", dep)
+        t_E = scopy(T.E[:], T.PA[:, 0:192], "E", [t_pa])
+        t_b = [tt(T.BT[:, 128:192], T.E[:, 128:192], T.E[:, 64:128], OP.is_gt, "b01", [t_E]),
+               tt(T.BT[:, 0:128], T.E[:, 0:128], T.PB[:, 0:128], OP.is_gt, "b23", [t_E, t_pb])]
+        t_ht = do("v", lambda: V.transpose(out=T.HT[:], in_=T.BT[:]), "HT", t_b)
+        if raw:
+            prep_cap(1)
+        for i, w, b in ((0, T.pmn, 128), (1, T.pmp, 128), (2, T.pmn, 0), (3, T.pmp, 0), (0, T.pmn, 64), (1, T.pmn, 64), (2, T.pmp, 64), (3, T.pmp, 64)):
+            mm(T.PH[:, i:256:4], w[:], T.HT[:, b:b + 64], False, False, "PH", [t_ht, t_pre[l]] + t_pm)
+        t_ph = mm(T.PH[:, 256:NV], T.pm5[:], T.HT[:, 64:96], False, True, "PH", [])
+        for j, (a0, a1, ld) in enumerate(PIECES):
+            b, P = (l - 1) * A, T["P%d" % j]
+            mm(P[:, 0:a1 - a0], T.idn[:], T.ST[:, b + a0:b + a1], True, False, None, [t_idn, t_st[l]] + t_ev)
+            mm(P[:, 0:a1 - a0], T["e%d" % ld][:], T.MC[:, b + a0:b + a1], False, False, None, [t_e[ld]] + t_mc[l])
+        t_sc = do("v", lambda: V.tensor_tensor_scan(out=T.SC[:], data0=T.RS[:], data1=T.PH[:, 0:256], initial=0.0, op0=OP.add, op1=OP.max), "SC", [t_ph, t_rs])
+        t_selm = vcopy(T.sel[:, 64:96], T.PH[:, 256:NV], "selm", [t_ph])
+        t_sel = vcopy(T.sel[:, 0:64], T.SC[:, 3:256:4], "sel", [t_sc])
+        h0, h1, ha, hb_ = (0, 256), (256, 512), (256, 384), (384, 512)
+        t_c = {}
+        for s, (a0, a1) in [(0, h0), (0, h1), (1, h0), (1, h1), (2, h0), (2, ha), (2, hb_)]:
+            b = (l - 1) * A
+            if s == 0:
+                prev, dep = (T.C1 if a1 <= H else T.C2)[:, b + a0:b + a1], t_cap[l] + [t_selm]
+            else:
+                prev, dep = XX[(s + 1) % 2][:, a0:a1], [t_sel] + [t_c[k] for k in t_c if k[0] == s - 1 and k[1] < a1 and a0 < k[2]]
+            wn, o = ((MN[:, 0:2 * A], 64), (win, 32), (win, 0))[s]
+            t_c[(s, a0, a1)] = tt(XX[s % 2][:, a0:a1], wn.indirect(T.sel[:, o + a0 // 16:o + a1 // 16]), prev, OP.min, "c%d_%d_%d" % (s, a0, a1), dep)
+        out, o0 = (T.YB, 0) if l == L else (T.W, first(l))
+        t_ev = []
+        for j, (a0, a1, ld) in enumerate(PIECES):
+            P, w = T["P%d" % j], T[("sb%d" if raw else "sf%d") % ld]
+            t_p = mm(P[:, 0:a1 - a0], w[:], XX[0][:, a0:a1], False, True, "sh%d" % j, [t_c[(2, a0, a1)], t_s[ld] if raw else t_sf[ld]])
+            t_ev.append(scopy(out[:, o0 + a0:o0 + a1], P[:, 0:a1 - a0], "ev%d" % j, [t_p]))
+        if l == L:
+            break
+        B = first(l)
+        t_own = hand_over(T.W[:, B:B + A], T.hand16, (l - 1) * 32, SA, T["SH%d" % l], T.W, B + A, l, t_ev + [t_hand16])
+        t_pl = prep_first(l + 1)
+        if raw:
+            m = M + N * SR
+            t_conv += [scopy(T.W[:, M // 2:m - 512], T.WB[:, M // 2:m - 512], "convs2", []), vcopy(T.W[:, m - 512:m], T.WB[:, m - 512:m], "convv2", [])]
+        prep_lists(l + 1)
+        prep_offsets(l + 1, t_pl)
+        prep_cap(l + 1)
+        ready = t_ev + t_conv + [t_own, ("arr%d" % l, landed)]
+    dma("y", T.y[:, 0:H], T.YB[:, 0:H], "y0", [t_ev[0]])
+    dma("y", T.y[:, H:A], T.YB[:, H:A], "y1", t_ev[1:])
+    for k in range(3):
+        wait("g", ("loc%d" % k, landed))
+    for name in total:
+        if best.get(name, 0) < total[name]:
+            wait("g", (name, total[name]))

@@ -5,6 +5,7 @@ from concourse.mybir import AluOpType as OP, ActivationFunctionType as AF
 M, A, L, SR, SA, N = 2048, 512, 3, 128, 64, 8
 H = A // 2
 PEN = 8192.0
+HUGE = 2.0 ** 80
 
 
 def first(l):
@@ -12,39 +13,41 @@ def first(l):
 
 
 BF, F32, I32, U16 = "bfloat16", "float32", "int32", "uint16"
-NV = 288
 SCRATCH = {
     "WB": ("sbuf", [128, M + N * SR], BF),
     "W": ("sbuf", [128, first(L)], F32),
     "shipi": ("sbuf", [128, 64], I32), "handi": ("sbuf", [128, 64], I32),
     "ship16": ("sbuf", [128, 64], U16), "hand16": ("sbuf", [128, 64], U16),
     "PT": ("sbuf", [128, 768], I32), "cu": ("sbuf", [128, 384], U16),
-    "CF": ("sbuf", [128, 128], F32), "TL": ("sbuf", [128, 128], F32), "VB": ("sbuf", [128, L * NV], F32),
+    "CF": ("sbuf", [128, 2, 4, 32], F32), "TL": ("sbuf", [128, 4, 2, 16], F32),
     "SB": ("sbuf", [128, N * SR], BF), "SH1": ("sbuf", [128, N * SA], F32), "SH2": ("sbuf", [128, N * SA], F32),
-    "GB": ("sbuf", [128, 2 * A], BF), "MB": ("sbuf", [128, 2 * A], BF), "GF": ("sbuf", [128, 2 * A], F32), "MF": ("sbuf", [128, 2 * A], F32),
-    "E": ("sbuf", [128, 192], F32), "BT": ("sbuf", [128, 192], BF), "HT": ("sbuf", [128, 192], BF),
-    "SC": ("sbuf", [128, 256], F32), "RS": ("sbuf", [128, 256], F32), "sel": ("sbuf", [128, 96], U16),
-    "XB0": ("sbuf", [128, A], BF), "XB1": ("sbuf", [128, A], BF), "XF0": ("sbuf", [128, A], F32), "XF1": ("sbuf", [128, A], F32),
-    "C1": ("sbuf", [128, L * A], BF), "C2": ("sbuf", [128, L * A], BF), "MC": ("sbuf", [128, L * A], BF), "ST": ("sbuf", [128, L * A], BF),
+    "BT": ("sbuf", [128, 3, 128], BF), "SC": ("sbuf", [128, 256], F32), "RS": ("sbuf", [128, 256], F32),
+    "CP": ("sbuf", [128, L * A], BF), "ST": ("sbuf", [128, L * A], BF), "CK": ("sbuf", [128, L * A], F32),
     "YB": ("sbuf", [128, A], F32),
-    "dist": ("sbuf", [128, 128], I32), "dm": ("sbuf", [128, 128], I32), "dmb": ("sbuf", [128, 128], I32), "m16": ("sbuf", [128, 128], I32),
-    "bit4": ("sbuf", [128, 128], I32), "dp": ("sbuf", [128, 128], I32), "dq": ("sbuf", [128, 32], I32), "pos": ("sbuf", [128, 32], I32), "posm": ("sbuf", [128, 32], I32),
-    "a1": ("sbuf", [128, 128], BF), "a2": ("sbuf", [128, 128], BF), "k1": ("sbuf", [128, 128], BF), "k2": ("sbuf", [128, 128], BF),
-    "sb1": ("sbuf", [128, 128], BF), "sb2": ("sbuf", [128, 128], BF), "sf1": ("sbuf", [128, 128], F32), "sf2": ("sbuf", [128, 128], F32),
-    "e1": ("sbuf", [128, 128], BF), "e2": ("sbuf", [128, 128], BF), "idn": ("sbuf", [128, 128], BF), "idf": ("sbuf", [128, 128], F32),
+    "xi": ("sbuf", [128, 128], I32), "dist": ("sbuf", [128, 128], I32), "dq": ("sbuf", [128, 96], I32),
+    "dc": ("sbuf", [128, 64, 4], I32), "dcm": ("sbuf", [128, 64, 4], I32), "pos": ("sbuf", [128, 32], I32), "posm": ("sbuf", [128, 32], I32),
+    "posf": ("sbuf", [128, 32], F32),
+    "sb1": ("sbuf", [128, 8, 16], BF), "sb2": ("sbuf", [128, 8, 16], BF), "sf1": ("sbuf", [128, 128], F32), "sf2": ("sbuf", [128, 128], F32),
+    "idn": ("sbuf", [128, 128], BF), "idf": ("sbuf", [128, 128], F32),
     "x00": ("sbuf", [128, 128], F32), "x01": ("sbuf", [128, 128], F32), "x10": ("sbuf", [128, 128], F32), "x11": ("sbuf", [128, 128], F32),
-    "pmp": ("sbuf", [128, 128], BF), "pmn": ("sbuf", [128, 128], BF), "pm5": ("sbuf", [128, 128], BF),
-    "qb": ("sbuf", [128, 32], BF), "qf": ("sbuf", [128, 32], F32),
-    "PA": ("psum", [128, 512], F32), "PB": ("psum", [128, 512], F32), "PH": ("psum", [128, 512], F32), "PL": ("psum", [128, 512], F32),
-    "P0": ("psum", [128, 512], F32), "P1": ("psum", [128, 512], F32), "P2": ("psum", [128, 512], F32),
+    "qb": ("sbuf", [128, 96], BF), "qf": ("sbuf", [128, 96], F32), "ZR": ("sbuf", [128, 384], BF), "TH": ("sbuf", [128, 128], BF),
+    "CN": ("sbuf", [128, 64, 4], BF), "pp": ("sbuf", [128, 64, 4], BF), "pa": ("sbuf", [128, 64, 2], BF), "pm": ("sbuf", [128, 32], BF),
+    "PD": ("psum", [128, 32, 16], F32), "PH": ("psum", [128, 512], F32), "PM": ("psum", [128, 512], F32), "PL": ("psum", [128, 512], F32),
+    "PK": ("psum", [128, 512], F32), "P0": ("psum", [128, 512], F32), "P1": ("psum", [128, 512], F32), "P2": ("psum", [128, 512], F32),
 }
+for _l in range(1, L + 1):
+    _t = BF if _l == 1 else F32
+    SCRATCH.update({"G%d" % _l: ("sbuf", [128, 2 * A], _t), "MN%d" % _l: ("sbuf", [128, 2 * A], _t), "sel%d" % _l: ("sbuf", [128, 96], U16),
+                    "XA%d" % _l: ("sbuf", [128, A], _t), "XB%d" % _l: ("sbuf", [128, A], _t), "XC%d" % _l: ("sbuf", [128, A], _t)})
 NPOOL = 140
 SEMAPHORES = ["arr0", "arr1", "arr2", "loc0", "loc1", "loc2"] + ["s%d" % i for i in range(NPOOL)]
 PIECES = [(0, 256, 1), (256, 384, 2), (384, 512, 2)]
 ON_S = [(0, 0, 128), (0, 128, 256), (0, 256, 512), (1, 0, 256), (1, 256, 512)]
 ON_V = [(0, 0, 128), (0, 128, 256), (0, 256, 512), (1, 0, 256), (1, 256, 384), (1, 384, 512)]
+ON_C = [("B", 0), ("B", 1), ("C", 0), ("B", 2), ("C", 1), ("C", 2)]
 BLOCKS = [("G", 0, 0), ("M", 0, 0), ("G", 0, 1), ("M", 0, 1), ("G", 0, 2), ("G", 0, 3), ("M", 0, 2), ("M", 0, 3),
           ("G", 1, 0), ("G", 1, 1), ("G", 1, 2), ("G", 1, 3), ("M", 1, 0), ("M", 1, 1), ("M", 1, 2), ("M", 1, 3)]
+DIFFS = {("G", 0): (0, 8, 64, 96), ("M", 0): (0, 16, 32, 96), ("G", 1): (16, 24, 64, 96), ("M", 1): (8, 24, 0, 64)}
 
 
 def rank_program(g, core, T, topo):
@@ -83,6 +86,12 @@ def rank_program(g, core, T, topo):
     def ts(out, a, s1, op, role, deps):
         return do("v", lambda: V.tensor_scalar(out=out, in0=a, scalar1=s1, scalar2=None, op0=op), role, deps)
 
+    def where(out, a, v, c, role, deps):
+        return do("v", lambda: V.tensor_scalar(out=out, in0=a, scalar1=v, scalar2=c, op0=OP.is_equal, op1=OP.mult), role, deps)
+
+    def fill(out, c, role, deps=()):
+        return do("v", lambda: V.memset(out, c), role, deps)
+
     def vcopy(out, a, role, deps):
         return do("v", lambda: V.tensor_copy(out=out, in_=a), role, deps)
 
@@ -95,8 +104,8 @@ def rank_program(g, core, T, topo):
     def dma(q, out, in_, role, deps=()):
         return do(q, lambda: Q[q].dma_start(out=out, in_=in_), role, deps, 16)
 
-    def iota(out, pat, base, cm, role):
-        return do("g", lambda: g.iota(out, pat, base, cm), role, [])
+    def iota(out, pat, base, cm, role, **kw):
+        return do("g", lambda: g.iota(out, pat, base, cm, **kw), role, [])
 
     here = topo.cores_of(core)
     far = [r for r in range(N) if topo.host(T.cores[r]) != topo.host(core)]
@@ -144,7 +153,7 @@ def rank_program(g, core, T, topo):
             return got
         h = len(far) // 2
         t1 = pick("v", far[:h], "f") + pick("s", far[h:], "f")
-        t2 = pick("v", near, "n") + pick("s", buddy, "b")
+        t2 = pick("v", near[:1], "n") + pick("s", near[1:], "n") + pick("v", buddy, "b")
         own = scopy(dst[:, w_dst + rank * per:w_dst + (rank + 1) * per], win.indirect(lists[:, col0 + rank * per16:col0 + (rank + 1) * per16]), "handown", deps)
         send(far, stage, dst, per, w_dst, k, t1)
         send(near + buddy, stage, dst, per, w_dst, k, t2)
@@ -155,96 +164,90 @@ def rank_program(g, core, T, topo):
     t_pt = {1: dma("s", T.PT[:, 0:256], T.parts[:, 0:256], "pt1")}
     t_hand = dma("s", T.handi[:], T.hand[:], "hand")
 
-    t_dist = iota(T.dist[:], [[1, 128]], 128, -1, "dist")
-    t_bit = iota(T.bit4[:], [[0, 4], [128, 2], [0, 16]], 0, 0, "bit4")
-    t_dp = iota(T.dp[:], [[-4, 8], [-1, 4], [-32, 4]], 0, 1, "dp")
-    t_dq = iota(T.dq[:], [[0, 4], [-16, 8]], -15, 1, "dq")
-    t_m16 = iota(T.m16[:], [[0, 8], [1, 16]], 0, 0, "m16")
+    t_xi = iota(T.xi[:], [[-32, 4], [1000, 2], [-1, 16]], 0, 1, "xi")
+    t_dq = iota(T.dq[:], [[0, 3], [-16, 8], [0, 4]], -15, 1, "dq")
+    t_dist = iota(T.dist[:], [[1, 128]], 0, -1, "dist")
+    t_dc = iota(T.dc[:], [[0, 2], [-1, 32], [0, 4]], 128, 1, "dc")
     t_pos = iota(T.pos[:], [[1, 32]], 0, 32, "pos")
-    t_r0 = do("v", lambda: V.memset(T.RS[:], 0.0), "rs0", [])
-    t_rs = do("v", lambda: V.memset(T.RS[:, 0:256:4], -1048576.0), "rs", [t_r0])
-    t_dm = ts(T.dm[:], T.dist[:], 127, OP.bitwise_and, "dm", [t_dist])
-    t_dmb = tt(T.dmb[:], T.dm[:], T.bit4[:], OP.add, "dmb", [t_dm, t_bit])
-    t_x = [ts(T[n][:], T.dmb[:], v, OP.is_equal, n, [t_dmb]) for n, v in (("x00", 0), ("x11", 128), ("x01", 144), ("x10", 112))]
+    t_cn = [iota(T.CN[:, 0:32, :], [[0, 32], [-int(PEN), 2], [int(PEN), 2]], -int(PEN), 0, "cn0", allow_small_or_imprecise_dtypes=True),
+            iota(T.CN[:, 32:64, :], [[0, 32], [-int(PEN), 2], [-int(PEN), 2]], 0, 0, "cn1", allow_small_or_imprecise_dtypes=True)]
+    t_rs = fill(T.RS[:, 0:256:4], -1048576.0, "rs", [fill(T.RS[:], 0.0, "rs0")])
+    t_zr = fill(T.ZR[:], 0.0, "zr")
+    t_th0 = fill(T.TH[:], HUGE, "th0")
+    t_x = [ts(T["x%d%d" % (hb, e)][:], T.xi[:], 16 * hb + 1000 * e, OP.is_equal, "x%d%d" % (hb, e), [t_xi]) for hb in range(2) for e in range(2)]
     X = [[T.x00, T.x01], [T.x10, T.x11]]
-    t_idn = ts(T.idn[:], T.dm[:], 0, OP.is_equal, "idn", [t_dm])
-    t_pm = [do("v", lambda: V.tensor_scalar(out=T[n][:], in0=T.dp[:], scalar1=0, scalar2=v, op0=OP.is_equal, op1=OP.mult), n, [t_dp])
-            for n, v in (("pmp", PEN), ("pmn", -PEN), ("pm5", -512.0))]
-    t_qb = ts(T.qb[:], T.dq[:], 0, OP.is_equal, "qb", [t_dq])
-    t_s, t_e, t_sf = {}, {}, {}
-    for ld in (1, 2):
-        ta = ts(T["a%d" % ld][:], T.dm[:], ld, OP.is_equal, "a%d" % ld, [t_dm])
-        tk = ts(T["k%d" % ld][:], T.m16[:], ld, OP.is_ge, "k%d" % ld, [t_m16])
-        t_s[ld] = tt(T["sb%d" % ld][:], T["a%d" % ld][:], T["k%d" % ld][:], OP.mult, "sb%d" % ld, [ta, tk])
-        t_e[ld] = tt(T["e%d" % ld][:], T["a%d" % ld][:], T["sb%d" % ld][:], OP.subtract, "e%d" % ld, [t_s[ld]])
-    t_posm = ts(T.posm[:], T.pos[:], 511, OP.bitwise_and, "posm", [t_pos])
+    for j in range(4):
+        t_th = fill(T.TH[32 * j:32 * j + 32, j:128:4], 0.0, "th", [t_th0])
+    t_qb = [where(T.qb[:, 0:64], T.dq[:, 0:64], 0, -1.0, "qb0", [t_dq]), where(T.qb[:, 64:96], T.dq[:, 64:96], 0, 1.0, "qb1", [t_dq])]
+    t_idn = ts(T.idn[:], T.dist[:], 0, OP.is_equal, "idn", [t_dist])
+    t_dcm = ts(T.dcm[:], T.dc[:], 31, OP.bitwise_and, "dcm", [t_dc])
     t_idf = scopy(T.idf[:], T.idn[:], "idf", [t_idn])
-    t_qf = scopy(T.qf[:], T.qb[:], "qf", [t_qb])
+    t_qf = [scopy(T.qf[:], T.qb[:], "qf", t_qb)]
 
     t_ship16 = vcopy(T.ship16[:], T.shipi[:], "ship16", [t_ship])
     t_own = hand_over(T.WB[:, 0:M], T.ship16, 0, SR, T.SB, T.WB, M, 0, [t_ship16, t_sup])
 
     wait("y", ("loc0", landed))
-    t_cap, t_st = {}, {}
-    wr = [dma("y", T.C1[127:128, :], T.cap[0:1, :], "capw1"), dma("y", T.C2[126:128, :], T.cap[0:2, :], "capw2")]
-
-    def load_cap(l):
-        b = (l - 1) * A
-        t_cap[l] = wr + [dma("y", T.C1[0:127, b:b + H], T.cap[1:128, b:b + H], "cap1_%d" % l),
-                         dma("y", T.C2[0:126, b + H:b + A], T.cap[2:128, b + H:b + A], "cap2_%d" % l)]
-    load_cap(1)
-    t_st[1] = dma("y", T.ST[:, 0:A], T.stock[:, 0:A], "st1")
+    t_cs = {1: [dma("y", T.CP[:, 0:A], T.cap[:, 0:A], "cp1"), dma("y", T.ST[:, 0:A], T.stock[:, 0:A], "st1")]}
     t_pt[2] = t_pt[3] = dma("y", T.PT[:, 256:768], T.parts[:, 256:768], "pt2")
-    load_cap(2)
-    load_cap(3)
-    t_st[2] = t_st[3] = dma("y", T.ST[:, A:3 * A], T.stock[:, A:3 * A], "st2")
+    t_cs[2] = t_cs[3] = [dma("y", T.CP[:, A:3 * A], T.cap[:, A:3 * A], "cp2"), dma("y", T.ST[:, A:3 * A], T.stock[:, A:3 * A], "st2")]
 
-    t_cu, t_pre, t_mc = {}, {}, {}
+    t_cu, t_pre, t_ck = {}, {}, {}
+    free = {"PD": [], "PH": [], "PM": [], "PL": [], "PK": [], "P": [], "CF": []}
 
-    def prep_first(l):
-        b = (l - 1) * 256
-        t_cf = vcopy(T.CF[:], T.PT[:, b:b + 128], "CF", [t_pt[l]])
-        t_tl = do("v", lambda: V.transpose(out=T.TL[:], in_=T.CF[:]), "TL", [t_cf])
-        for i in range(4):
-            for hb in range(2):
-                for e in range(2):
-                    t_pl = mm(T.PL[:, i * 32 + hb:(i + 1) * 32:2], X[hb][e][:], T.TL[:, i * 32 + 16 * e:i * 32 + 16 * e + 16], e == 0, e == 1, "PL", t_x + [t_tl])
-        return t_pl
-
-    def prep_offsets(l, t_pl):
-        c = (l - 1) * 128
+    def prep_lists(l, more):
+        b, c = (l - 1) * 256, (l - 1) * 128
+        t_cf = vcopy(T.CF[:], T.PT[:, b:b + 256], "CF", [t_pt[l]] + free["CF"])
+        t_tl = do("v", lambda: V.transpose(out=T.TL[:], in_=T.CF[:, 0]), "TL", [t_cf])
+        for hb in range(2):
+            for e in range(2):
+                t_pl = mm(T.PL[:, hb:128:2], X[hb][e][:], T.TL[:, :, e, :], e == 0, e == 1, "PL", t_x + [t_tl] + free["PL"])
+        t_posf = more()
         t_cu[l] = vcopy(T.cu[:, c:c + 128], T.PL[:, 0:128], "cu", [t_pl])
+        free["PL"] = [t_cu[l]]
+        mm(T.PD[:, 0:24, :], T.idn[:], T.ZR[:], True, False, None, [t_idn, t_zr] + free["PD"])
+        mm(T.PH[:, 0:256], T.idn[:], T.CN[:], True, False, None, t_cn + free["PH"])
+        for i in range(4):
+            t = mm(T.PH[:, i:256:4], T.idf[:], T.CF[:, :, i, :], False, False, "pre", [t_idf])
+        free["CF"] = [t]
+        mm(T.PM[:, 0:32], T.idf[:], T.posf[:], True, False, None, [t_posf] + free["PM"])
 
-    def prep_lists(l):
-        b, o = (l - 1) * 256, (l - 1) * NV
-        got = []
-        for i, pen in enumerate((0.0, -PEN, -PEN, -2 * PEN)):
-            for k, p in ((0, b + (i ^ 1) * 32), (1, b + 128 + i * 32)):
-                got.append(ts(T.VB[:, o + k * 128 + i:o + (k + 1) * 128:4], T.PT[:, p:p + 32], pen, OP.add, "vb%d%d" % (k, i), [t_pt[l]]))
-        got.append(ts(T.VB[:, o + 256:o + NV], T.posm[:], 512.0, OP.add, "vbm", [t_posm]))
-        t_pre[l] = mm(T.PH[:, 0:NV], T.idf[:], T.VB[:, o:o + NV], True, False, "pre", got + [t_idf])
-
-    def prep_cap(l):
+    def prep_sums(l):
         b = (l - 1) * A
-        t_mc[l] = [ts(T.MC[:, b:b + H], T.C1[:, b:b + H], 0.0, OP.min, "mc1", t_cap[l]),
-                   ts(T.MC[:, b + H:b + A], T.C2[:, b + H:b + A], 0.0, OP.min, "mc2", t_cap[l])]
+        for j, (a0, a1, ld) in enumerate(PIECES):
+            mm(T["P%d" % j][:, 0:a1 - a0], T.idn[:], T.ST[:, b + a0:b + a1], True, False, None, t_cs[l] + free["P"])
+        mm(T.PK[:], T.idn[:], T.CP[:, b:b + A], True, False, None, free["PK"])
+        return mm(T.PK[:], T.idn[:], T.ST[:, b:b + A], False, True, "PK", [])
 
-    t_pl = prep_first(1)
-    prep_lists(1)
-    prep_offsets(1, t_pl)
+    def take_sums(l, t):
+        t_ck[l] = scopy(T.CK[:, (l - 1) * A:l * A], T.PK[:], "CK", [t])
+        free["PK"] = [t_ck[l]]
+
+    got = {}
+
+    def more_constants():
+        t = ts(T.posm[:], T.pos[:], 511, OP.bitwise_and, "posm", [t_pos])
+        got["pp"] = [where(T.pp[:, :, 0:2], T.dcm[:, :, 0:2], 0, -PEN, "pp0", [t_dcm]), where(T.pp[:, :, 2:4], T.dcm[:, :, 2:4], 0, PEN, "pp1", [t_dcm])]
+        got["posf"] = ts(T.posf[:], T.posm[:], float(A), OP.add, "posf", [t])
+        return got["posf"]
+    prep_lists(1, more_constants)
+    t_pp = got["pp"]
+    t_pa = [ts(T.pa[:, 0:32, :], T.pp[:, 0:32, 1:3], -1.0, OP.mult, "pa0", t_pp), vcopy(T.pa[:, 32:64, :], T.pp[:, 0:32, 1:3], "pa1", t_pp)]
+    t_pm = ts(T.pm[:], T.pp[:, 0:32, 0], A / PEN, OP.mult, "pm", t_pp)
+    t_s, t_sf = {}, {}
+    for ld in (1, 2):
+        t_s[ld] = ts(T["sb%d" % ld][:], T.dist[:], ld, OP.is_equal, "sa%d" % ld, [t_dist])
     t_hand16 = vcopy(T.hand16[:], T.handi[:], "hand16", [t_hand])
     for ld in (1, 2):
-        t_sf[ld] = scopy(T["sf%d" % ld][:], T["sb%d" % ld][:], "sf%d" % ld, [t_s[ld]])
-    t_conv = [scopy(T.W[:, 0:M // 2], T.WB[:, 0:M // 2], "convs", [])]
+        t_s[ld] = fill(T["sb%d" % ld][:, :, 0:ld], 0.0, "sb%d" % ld, [t_s[ld]])
+    t_conv = [scopy(T.W[:, 0:M // 2], T.WB[:, 0:M // 2], "conv0", []), scopy(T.W[:, M // 2:M], T.WB[:, M // 2:M], "conv1", [])]
 
     ready = [t_own, t_sup, ("arr0", landed)]
-    t_ev = []
     for l in range(1, L + 1):
         raw = l == 1
         win = (T.WB if raw else T.W)[:, 0:first(l)]
-        G, MN = (T.GB, T.MB) if raw else (T.GF, T.MF)
-        XX = (T.XB0, T.XB1) if raw else (T.XF0, T.XF1)
-        c = (l - 1) * 128
+        G, MN, sel, XA, XB, XC = (T["%s%d" % (n, l)] for n in ("G", "MN", "sel", "XA", "XB", "XC"))
+        c, b = (l - 1) * 128, (l - 1) * A
         t_g, t_m = {}, {}
         for p, a0, a1 in ON_S:
             li = T.cu[:, c + 2 * p * 32 + a0 // 16:c + 2 * p * 32 + a1 // 16]
@@ -253,62 +256,58 @@ def rank_program(g, core, T, topo):
             li = T.cu[:, c + (2 * p + 1) * 32 + a0 // 16:c + (2 * p + 1) * 32 + a1 // 16]
             t_m[(p, a0, a1)] = tt(MN[:, p * A + a0:p * A + a1], win.indirect(li), G[:, p * A + a0:p * A + a1], OP.min, "m%d_%d" % (p, a0),
                                   ready + [t_cu[l]] + [t_g[k] for k in t_g if k[0] == p and k[1] < a1 and a0 < k[2]])
-        q = T.qb if raw else T.qf
-        for kind, p, y in BLOCKS:
+        q, t_q = (T.qb, t_qb) if raw else (T.qf, t_qf)
+        for n, (kind, p, y) in enumerate(BLOCKS):
             toks, src = (t_g, G) if kind == "G" else (t_m, MN)
-            dep = [toks[k] for k in toks if k[0] == p and k[1] <= 128 * y < k[2]] + [t_qb if raw else t_qf]
-            w = src[:, p * A + 128 * y:p * A + 128 * y + 128]
-            if (kind, p) == ("M", 1):
-                t_pb = mm(T.PB[:, y:128:4], w, q[:, 0:32], True, True, "PB", dep)
-            else:
-                o = {("G", 1): 0, ("M", 0): 64, ("G", 0): 128}[(kind, p)]
-                t_pa = mm(T.PA[:, o + y:o + 64:4], w, q[:, 0:16], True, True, "PA", dep)
-        t_E = scopy(T.E[:], T.PA[:, 0:192], "E", [t_pa])
-        t_b = [tt(T.BT[:, 128:192], T.E[:, 128:192], T.E[:, 64:128], OP.is_gt, "b01", [t_E]),
-               tt(T.BT[:, 0:128], T.E[:, 0:128], T.PB[:, 0:128], OP.is_gt, "b23", [t_E, t_pb])]
-        t_ht = do("v", lambda: V.transpose(out=T.HT[:], in_=T.BT[:]), "HT", t_b)
+            r0, r1, q0, q1 = DIFFS[(kind, p)]
+            t_pd = mm(T.PD[:, r0:r1, 4 * y:4 * y + 4], src[:, p * A + 128 * y:p * A + 128 * y + 128], q[:, q0:q1], False, n == len(BLOCKS) - 1, "PD",
+                      [toks[k] for k in toks if k[0] == p and k[1] <= 128 * y < k[2]] + t_q)
         if raw:
-            prep_cap(1)
-        for i, w, b in ((0, T.pmn, 128), (1, T.pmp, 128), (2, T.pmn, 0), (3, T.pmp, 0), (0, T.pmn, 64), (1, T.pmn, 64), (2, T.pmp, 64), (3, T.pmp, 64)):
-            mm(T.PH[:, i:256:4], w[:], T.HT[:, b:b + 64], False, False, "PH", [t_ht, t_pre[l]] + t_pm)
-        t_ph = mm(T.PH[:, 256:NV], T.pm5[:], T.HT[:, 64:96], False, True, "PH", [])
-        for j, (a0, a1, ld) in enumerate(PIECES):
-            b, P = (l - 1) * A, T["P%d" % j]
-            mm(P[:, 0:a1 - a0], T.idn[:], T.ST[:, b + a0:b + a1], True, False, None, [t_idn, t_st[l]] + t_ev)
-            mm(P[:, 0:a1 - a0], T["e%d" % ld][:], T.MC[:, b + a0:b + a1], False, False, None, [t_e[ld]] + t_mc[l])
+            t_conv.append(scopy(T.W[:, M:M + A], T.WB[:, M:M + A], "conv2", []))
+        def bits(j):
+            return tt(T.BT[:, j], T.PD[:, 8 * j:8 * j + 8, :], T.TH[:], OP.is_gt, "b%d" % j, [t_pd, t_th])
+        t_bp, t_b01, t_b23 = bits(1), bits(0), bits(2)
+        t_pos2 = mm(T.PM[:, 0:32], T.BT[:, 1], T.pm[:], False, True, "PM", [t_bp, t_pm])
+        t_selm = vcopy(sel[:, 64:96], T.PM[:, 0:32], "selm", [t_pos2])
+        mm(T.PH[:, 0:256], T.BT[:, 1], T.pp[:], False, False, None, t_pp)
+        for i in range(4):
+            t_ph = mm(T.PH[:, i:256:4], T.BT[:, i & 2], T.pa[:, :, i & 1], False, i == 3, "PH", [t_b23 if i & 2 else t_b01] + t_pa)
         t_sc = do("v", lambda: V.tensor_tensor_scan(out=T.SC[:], data0=T.RS[:], data1=T.PH[:, 0:256], initial=0.0, op0=OP.add, op1=OP.max), "SC", [t_ph, t_rs])
-        t_selm = vcopy(T.sel[:, 64:96], T.PH[:, 256:NV], "selm", [t_ph])
-        t_sel = vcopy(T.sel[:, 0:64], T.SC[:, 3:256:4], "sel", [t_sc])
-        h0, h1, ha, hb_ = (0, 256), (256, 512), (256, 384), (384, 512)
-        t_c = {}
-        for s, (a0, a1) in [(0, h0), (0, h1), (1, h0), (1, h1), (2, h0), (2, ha), (2, hb_)]:
-            b = (l - 1) * A
-            if s == 0:
-                prev, dep = (T.C1 if a1 <= H else T.C2)[:, b + a0:b + a1], t_cap[l] + [t_selm]
+        t_sel = vcopy(sel[:, 0:64], T.SC[:, 3:256:4], "sel", [t_sc])
+        free.update(PD=[t_b23], PH=[t_sc], PM=[t_selm])
+        if raw:
+            t_pk = prep_sums(l)
+        t_a = {k: scopy(XA[:, k[0]:k[1]], MN[:, 0:2 * A].indirect(sel[:, 64 + k[0] // 16:64 + k[1] // 16]), "xa%d" % k[0], [t_selm]) for k in ((0, H), (H, A))}
+        t_b, t_c = {}, {}
+        for s, j in ON_C:
+            a0, a1 = PIECES[j][0:2]
+            if s == "B":
+                t_b[j] = tt(XB[:, a0:a1], win.indirect(sel[:, a0 // 16:a1 // 16]), XA[:, a0:a1], OP.min, "xb%d" % j, [t_sel, t_a[(0, H) if a0 < H else (H, A)]])
             else:
-                prev, dep = XX[(s + 1) % 2][:, a0:a1], [t_sel] + [t_c[k] for k in t_c if k[0] == s - 1 and k[1] < a1 and a0 < k[2]]
-            wn, o = ((MN[:, 0:2 * A], 64), (win, 32), (win, 0))[s]
-            t_c[(s, a0, a1)] = tt(XX[s % 2][:, a0:a1], wn.indirect(T.sel[:, o + a0 // 16:o + a1 // 16]), prev, OP.min, "c%d_%d_%d" % (s, a0, a1), dep)
+                t_c[j] = tt(XC[:, a0:a1], win.indirect(sel[:, 32 + a0 // 16:32 + a1 // 16]), XB[:, a0:a1], OP.min, "xc%d" % j, [t_b[j]])
+        if raw:
+            take_sums(l, t_pk)
+            t_conv.append(scopy(T.W[:, M + A:M + 2 * A], T.WB[:, M + A:M + 2 * A], "conv3", []))
         out, o0 = (T.YB, 0) if l == L else (T.W, first(l))
         t_ev = []
         for j, (a0, a1, ld) in enumerate(PIECES):
             P, w = T["P%d" % j], T[("sb%d" if raw else "sf%d") % ld]
-            t_p = mm(P[:, 0:a1 - a0], w[:], XX[0][:, a0:a1], False, True, "sh%d" % j, [t_c[(2, a0, a1)], t_s[ld] if raw else t_sf[ld]])
-            t_ev.append(scopy(out[:, o0 + a0:o0 + a1], P[:, 0:a1 - a0], "ev%d" % j, [t_p]))
+            t_p = mm(P[:, 0:a1 - a0], w[:], XC[:, a0:a1], False, True, "sh%d" % j, [t_c[j], t_s[ld] if raw else t_sf[ld]])
+            t_ev.append(tt(out[:, o0 + a0:o0 + a1], P[:, 0:a1 - a0], T.CK[:, b + a0:b + a1], OP.min, "ev%d" % j, [t_p, t_ck[l]]))
+        free["P"] = t_ev
         if l == L:
             break
         B = first(l)
         t_own = hand_over(T.W[:, B:B + A], T.hand16, (l - 1) * 32, SA, T["SH%d" % l], T.W, B + A, l, t_ev + [t_hand16])
-        t_pl = prep_first(l + 1)
+        t_pk = prep_sums(l + 1)
+        prep_lists(l + 1, lambda: got["posf"])
         if raw:
-            m = M + N * SR
-            t_conv += [scopy(T.W[:, M // 2:m - 512], T.WB[:, M // 2:m - 512], "convs2", []), vcopy(T.W[:, m - 512:m], T.WB[:, m - 512:m], "convv2", [])]
-        prep_lists(l + 1)
-        prep_offsets(l + 1, t_pl)
-        prep_cap(l + 1)
+            for ld in (1, 2):
+                t_sf[ld] = scopy(T["sf%d" % ld][:], T["sb%d" % ld][:], "sf%d" % ld, [t_s[ld]])
+        take_sums(l + 1, t_pk)
         ready = t_ev + t_conv + [t_own, ("arr%d" % l, landed)]
-    dma("y", T.y[:, 0:H], T.YB[:, 0:H], "y0", [t_ev[0]])
-    dma("y", T.y[:, H:A], T.YB[:, H:A], "y1", t_ev[1:])
+    for j, (a0, a1, ld) in enumerate(PIECES):
+        dma("ysy"[j], T.y[:, a0:a1], T.YB[:, a0:a1], "y%d" % j, [t_ev[j]])
     for k in range(3):
         wait("g", ("loc%d" % k, landed))
     for name in total:

@@ -21,7 +21,7 @@ SCRATCH = {
     "PT": ("sbuf", [128, 768], I32), "cu": ("sbuf", [128, 384], U16),
     "CF": ("sbuf", [128, 2, 4, 32], F32), "TL": ("sbuf", [128, 4, 2, 16], F32),
     "SB": ("sbuf", [128, N * SR], BF), "SH1": ("sbuf", [128, N * SA], F32), "SH2": ("sbuf", [128, N * SA], F32),
-    "BT": ("sbuf", [128, 3, 128], BF), "SC": ("sbuf", [128, 256], F32), "RS": ("sbuf", [128, 256], F32),
+    "BT": ("sbuf", [128, 24, 16], BF), "SC": ("sbuf", [128, 256], F32), "RS": ("sbuf", [128, 128], F32),
     "CP": ("sbuf", [128, L * A], BF), "ST": ("sbuf", [128, L * A], BF), "CK": ("sbuf", [128, L * A], F32),
     "YB": ("sbuf", [128, A], F32),
     "xi": ("sbuf", [128, 128], I32), "dist": ("sbuf", [128, 128], I32), "dq": ("sbuf", [128, 96], I32),
@@ -30,9 +30,9 @@ SCRATCH = {
     "sb1": ("sbuf", [128, 8, 16], BF), "sb2": ("sbuf", [128, 8, 16], BF), "sf1": ("sbuf", [128, 128], F32), "sf2": ("sbuf", [128, 128], F32),
     "idn": ("sbuf", [128, 128], BF), "idf": ("sbuf", [128, 128], F32),
     "x00": ("sbuf", [128, 128], F32), "x01": ("sbuf", [128, 128], F32), "x10": ("sbuf", [128, 128], F32), "x11": ("sbuf", [128, 128], F32),
-    "qb": ("sbuf", [128, 96], BF), "qf": ("sbuf", [128, 96], F32), "ZR": ("sbuf", [128, 384], BF), "TH": ("sbuf", [128, 128], BF),
+    "qb": ("sbuf", [128, 96], BF), "qf": ("sbuf", [128, 96], F32), "ZR": ("sbuf", [128, 192], BF), "TH": ("sbuf", [128, 192], BF),
     "CN": ("sbuf", [128, 64, 4], BF), "pp": ("sbuf", [128, 64, 4], BF), "pa": ("sbuf", [128, 64, 2], BF), "pm": ("sbuf", [128, 32], BF),
-    "PD": ("psum", [128, 32, 16], F32), "PH": ("psum", [128, 512], F32), "PM": ("psum", [128, 512], F32), "PL": ("psum", [128, 512], F32),
+    "PD0": ("psum", [128, 64, 8], F32), "PD1": ("psum", [128, 64, 8], F32), "PH": ("psum", [128, 512], F32), "PL": ("psum", [128, 512], F32),
     "PK": ("psum", [128, 512], F32), "P0": ("psum", [128, 512], F32), "P1": ("psum", [128, 512], F32), "P2": ("psum", [128, 512], F32),
 }
 for _l in range(1, L + 1):
@@ -42,11 +42,12 @@ for _l in range(1, L + 1):
 NPOOL = 140
 SEMAPHORES = ["arr0", "arr1", "arr2", "loc0", "loc1", "loc2"] + ["s%d" % i for i in range(NPOOL)]
 PIECES = [(0, 256, 1), (256, 384, 2), (384, 512, 2)]
-ON_S = [(0, 0, 128), (0, 128, 256), (0, 256, 512), (1, 0, 256), (1, 256, 512)]
-ON_V = [(0, 0, 128), (0, 128, 256), (0, 256, 512), (1, 0, 256), (1, 256, 384), (1, 384, 512)]
+ON_A = [("v", "G", 1, 0, 128), ("s", "G", 0, 0, 128), ("s", "G", 0, 128, 256), ("s", "G", 1, 128, 256), ("s", "G", 0, 256, 512), ("s", "G", 1, 256, 384),
+        ("s", "G", 1, 384, 512), ("v", "M", 1, 0, 128), ("v", "M", 0, 0, 128), ("v", "M", 0, 128, 256), ("v", "M", 1, 128, 256), ("v", "M", 0, 256, 512),
+        ("v", "M", 1, 256, 384), ("v", "M", 1, 384, 512)]
 ON_C = [("B", 0), ("B", 1), ("C", 0), ("B", 2), ("C", 1), ("C", 2)]
-BLOCKS = [("G", 0, 0), ("M", 0, 0), ("G", 0, 1), ("M", 0, 1), ("G", 0, 2), ("G", 0, 3), ("M", 0, 2), ("M", 0, 3),
-          ("G", 1, 0), ("G", 1, 1), ("G", 1, 2), ("G", 1, 3), ("M", 1, 0), ("M", 1, 1), ("M", 1, 2), ("M", 1, 3)]
+BLOCKS = [("G", 1, 0), ("G", 0, 0), ("G", 0, 1), ("M", 1, 0), ("M", 0, 0), ("G", 1, 1), ("M", 0, 1), ("G", 0, 2), ("M", 1, 1),
+          ("G", 0, 3), ("G", 1, 2), ("G", 1, 3), ("M", 0, 2), ("M", 0, 3), ("M", 1, 2), ("M", 1, 3)]
 DIFFS = {("G", 0): (0, 8, 64, 96), ("M", 0): (0, 16, 32, 96), ("G", 1): (16, 24, 64, 96), ("M", 1): (8, 24, 0, 64)}
 
 
@@ -55,7 +56,7 @@ def rank_program(g, core, T, topo):
     if rank is None:
         return
     Q = {"v": g.vector, "s": g.scalar, "t": g.tensor, "g": g, "y": g.sync}
-    pool, total, seen, best = {}, {}, {q: {} for q in Q}, {}
+    pool, total, seen, best, before = {}, {}, {q: {} for q in Q}, {}, {}
 
     def wait(q, tok):
         name, val = tok
@@ -64,6 +65,8 @@ def rank_program(g, core, T, topo):
         Q[q].wait_ge(T.sem[name], val)
         seen[q][name] = val
         best[name] = max(best.get(name, 0), val)
+        for k, v in before.get(tok, {}).items():
+            seen[q][k] = max(seen[q].get(k, 0), v)
 
     def do(q, fn, role, deps, n=1):
         for d in deps:
@@ -76,6 +79,7 @@ def rank_program(g, core, T, topo):
         name = pool[role]
         inst.then_inc(T.sem[name], n)
         total[name] = total.get(name, 0) + n
+        before[(name, total[name])] = dict(seen[q])
         return (name, total[name])
 
     V, S, PE = g.vector, g.scalar, g.tensor
@@ -113,11 +117,12 @@ def rank_program(g, core, T, topo):
     near = [r for r in range(N) if r not in far and r not in buddy and r != rank]
     off = topo.engines(core, T.cores[far[0]])
     rest = [e for e in topo.engines(core, T.cores[buddy[0]]) if e not in off]
-    share = {}
-    for grp in (far, near):
-        k = len(off) // len(grp)
-        for j, r in enumerate(grp):
-            share[r] = off[j * k:(j + 1) * k]
+    plane = [r for r in far if topo.same_plane(core, T.cores[r])]
+    farthest = [r for r in far if r not in plane]
+    order = [r for grp in (farthest, plane, near) for r in sorted(grp, key=lambda r: topo.die(T.cores[r]) == topo.die(core))]
+    calls = [[r] for r in order]
+    calls[1] = calls[1] + buddy
+    share = {r: off for r in order}
     for j, r in enumerate(buddy):
         share[r] = rest[4 * j:4 * j + 4:2]
     landed = sum(len(v) for v in share.values())
@@ -133,31 +138,21 @@ def rank_program(g, core, T, topo):
                                         remote_sem=T.sem["arr%d" % k]))
         g.remote_dma_fused(tr, local_sem=T.sem["loc%d" % k])
 
-    def runs(ranks):
-        out = []
-        for r in ranks:
-            if out and out[-1][1] == r:
-                out[-1][1] = r + 1
-            else:
-                out.append([r, r + 1])
-        return out
-
     def hand_over(win, lists, col0, per, stage, dst, w_dst, k, deps):
         per16 = per // 16
 
-        def pick(q, ranks, tag):
-            got = []
-            for j, (b, e) in enumerate(runs(ranks)):
-                o, i = stage[:, b * per:e * per], win.indirect(lists[:, col0 + b * per16:col0 + e * per16])
-                got.append((vcopy if q == "v" else scopy)(o, i, "hand%s%s%d" % (q, tag, j), deps))
-            return got
-        h = len(far) // 2
-        t1 = pick("v", far[:h], "f") + pick("s", far[h:], "f")
-        t2 = pick("v", near[:1], "n") + pick("s", near[1:], "n") + pick("v", buddy, "b")
-        own = scopy(dst[:, w_dst + rank * per:w_dst + (rank + 1) * per], win.indirect(lists[:, col0 + rank * per16:col0 + (rank + 1) * per16]), "handown", deps)
-        send(far, stage, dst, per, w_dst, k, t1)
-        send(near + buddy, stage, dst, per, w_dst, k, t2)
-        return own
+        def pick(copy, b, e, tag):
+            return copy(stage[:, 16 * b:16 * e], win.indirect(lists[:, col0 + b:col0 + e]), "hand%d" % tag, deps)
+        for j, grp in enumerate(calls):
+            if j == 0:
+                b = grp[0] * per16
+                pick(vcopy, b, b + per16 // 2, j)
+                t = pick(scopy, b + per16 // 2, b + per16, j)
+            else:
+                for i, r in enumerate(grp):
+                    t = pick((scopy, vcopy)[(i + j) % 2], r * per16, (r + 1) * per16, j)
+            send(grp, stage, dst, per, w_dst, k, [t])
+        return scopy(dst[:, w_dst + rank * per:w_dst + (rank + 1) * per], win.indirect(lists[:, col0 + rank * per16:col0 + (rank + 1) * per16]), "handown", deps)
 
     t_sup = dma("y", T.WB[:, 0:M], T.sup[:], "sup")
     t_ship = dma("s", T.shipi[:], T.ship[:], "ship")
@@ -171,13 +166,13 @@ def rank_program(g, core, T, topo):
     t_pos = iota(T.pos[:], [[1, 32]], 0, 32, "pos")
     t_cn = [iota(T.CN[:, 0:32, :], [[0, 32], [-int(PEN), 2], [int(PEN), 2]], -int(PEN), 0, "cn0", allow_small_or_imprecise_dtypes=True),
             iota(T.CN[:, 32:64, :], [[0, 32], [-int(PEN), 2], [-int(PEN), 2]], 0, 0, "cn1", allow_small_or_imprecise_dtypes=True)]
-    t_rs = fill(T.RS[:, 0:256:4], -1048576.0, "rs", [fill(T.RS[:], 0.0, "rs0")])
+    t_rs = fill(T.RS[:, 0:128:4], -1048576.0, "rs", [fill(T.RS[:], 0.0, "rs0")])
     t_zr = fill(T.ZR[:], 0.0, "zr")
     t_th0 = fill(T.TH[:], HUGE, "th0")
     t_x = [ts(T["x%d%d" % (hb, e)][:], T.xi[:], 16 * hb + 1000 * e, OP.is_equal, "x%d%d" % (hb, e), [t_xi]) for hb in range(2) for e in range(2)]
     X = [[T.x00, T.x01], [T.x10, T.x11]]
     for j in range(4):
-        t_th = fill(T.TH[32 * j:32 * j + 32, j:128:4], 0.0, "th", [t_th0])
+        t_th = fill(T.TH[32 * j:32 * j + 32, j:192:4], 0.0, "th", [t_th0])
     t_qb = [where(T.qb[:, 0:64], T.dq[:, 0:64], 0, -1.0, "qb0", [t_dq]), where(T.qb[:, 64:96], T.dq[:, 64:96], 0, 1.0, "qb1", [t_dq])]
     t_idn = ts(T.idn[:], T.dist[:], 0, OP.is_equal, "idn", [t_dist])
     t_dcm = ts(T.dcm[:], T.dc[:], 31, OP.bitwise_and, "dcm", [t_dc])
@@ -204,13 +199,13 @@ def rank_program(g, core, T, topo):
                 t_pl = mm(T.PL[:, hb:128:2], X[hb][e][:], T.TL[:, :, e, :], e == 0, e == 1, "PL", t_x + [t_tl] + free["PL"])
         t_posf = more()
         t_cu[l] = vcopy(T.cu[:, c:c + 128], T.PL[:, 0:128], "cu", [t_pl])
-        free["PL"] = [t_cu[l]]
-        mm(T.PD[:, 0:24, :], T.idn[:], T.ZR[:], True, False, None, [t_idn, t_zr] + free["PD"])
+        for PD in (T.PD0, T.PD1):
+            mm(PD[:, 0:24, :], T.idn[:], T.ZR[:], True, False, None, [t_idn, t_zr] + free["PD"])
         mm(T.PH[:, 0:256], T.idn[:], T.CN[:], True, False, None, t_cn + free["PH"])
         for i in range(4):
             t = mm(T.PH[:, i:256:4], T.idf[:], T.CF[:, :, i, :], False, False, "pre", [t_idf])
         free["CF"] = [t]
-        mm(T.PM[:, 0:32], T.idf[:], T.posf[:], True, False, None, [t_posf] + free["PM"])
+        mm(T.PL[:, 128:160], T.idf[:], T.posf[:], True, False, None, [t_posf, t_cu[l]])
 
     def prep_sums(l):
         b = (l - 1) * A
@@ -248,33 +243,42 @@ def rank_program(g, core, T, topo):
         win = (T.WB if raw else T.W)[:, 0:first(l)]
         G, MN, sel, XA, XB, XC = (T["%s%d" % (n, l)] for n in ("G", "MN", "sel", "XA", "XB", "XC"))
         c, b = (l - 1) * 128, (l - 1) * A
-        t_g, t_m = {}, {}
-        for p, a0, a1 in ON_S:
-            li = T.cu[:, c + 2 * p * 32 + a0 // 16:c + 2 * p * 32 + a1 // 16]
-            t_g[(p, a0, a1)] = scopy(G[:, p * A + a0:p * A + a1], win.indirect(li), "g%d_%d" % (p, a0), ready + [t_cu[l]])
-        for p, a0, a1 in ON_V:
-            li = T.cu[:, c + (2 * p + 1) * 32 + a0 // 16:c + (2 * p + 1) * 32 + a1 // 16]
-            t_m[(p, a0, a1)] = tt(MN[:, p * A + a0:p * A + a1], win.indirect(li), G[:, p * A + a0:p * A + a1], OP.min, "m%d_%d" % (p, a0),
-                                  ready + [t_cu[l]] + [t_g[k] for k in t_g if k[0] == p and k[1] < a1 and a0 < k[2]])
+        t_a = {}
+        for qu, kind, p, a0, a1 in ON_A:
+            o = c + (2 * p + (kind == "M")) * 32
+            part = win.indirect(T.cu[:, o + a0 // 16:o + a1 // 16])
+            role, dep = "%s%d_%d" % (kind, p, a0), [t_cu[l]] + ready
+            if kind == "G":
+                t = (vcopy if qu == "v" else scopy)(G[:, p * A + a0:p * A + a1], part, role, dep)
+            else:
+                t = tt(MN[:, p * A + a0:p * A + a1], part, G[:, p * A + a0:p * A + a1], OP.min, role,
+                       dep + [t_a[k] for k in t_a if k[0:2] == ("G", p) and k[2] < a1 and a0 < k[3]])
+            t_a[(kind, p, a0, a1)] = t
         q, t_q = (T.qb, t_qb) if raw else (T.qf, t_qf)
+        t_pd = {}
         for n, (kind, p, y) in enumerate(BLOCKS):
-            toks, src = (t_g, G) if kind == "G" else (t_m, MN)
+            src = G if kind == "G" else MN
             r0, r1, q0, q1 = DIFFS[(kind, p)]
-            t_pd = mm(T.PD[:, r0:r1, 4 * y:4 * y + 4], src[:, p * A + 128 * y:p * A + 128 * y + 128], q[:, q0:q1], False, n == len(BLOCKS) - 1, "PD",
-                      [toks[k] for k in toks if k[0] == p and k[1] <= 128 * y < k[2]] + t_q)
+            t_pd[y // 2] = mm(T["PD%d" % (y // 2)][:, r0:r1, 4 * (y % 2):4 * (y % 2) + 4], src[:, p * A + 128 * y:p * A + 128 * y + 128], q[:, q0:q1],
+                              False, all(z // 2 != y // 2 for _, _, z in BLOCKS[n + 1:]), "PD%d" % (y // 2),
+                              [t_a[k] for k in t_a if k[0:2] == (kind, p) and k[2] <= 128 * y < k[3]] + t_q)
         if raw:
             t_conv.append(scopy(T.W[:, M:M + A], T.WB[:, M:M + A], "conv2", []))
-        def bits(j):
-            return tt(T.BT[:, j], T.PD[:, 8 * j:8 * j + 8, :], T.TH[:], OP.is_gt, "b%d" % j, [t_pd, t_th])
-        t_bp, t_b01, t_b23 = bits(1), bits(0), bits(2)
-        t_pos2 = mm(T.PM[:, 0:32], T.BT[:, 1], T.pm[:], False, True, "PM", [t_bp, t_pm])
-        t_selm = vcopy(sel[:, 64:96], T.PM[:, 0:32], "selm", [t_pos2])
-        mm(T.PH[:, 0:256], T.BT[:, 1], T.pp[:], False, False, None, t_pp)
+
+        def bits(h, j0, j1):
+            return tt(T.BT[:, 8 * j0:8 * j1, 8 * h:8 * h + 8], T["PD%d" % h][:, 8 * j0:8 * j1, :], T.TH[:, 0:64 * (j1 - j0)], OP.is_gt,
+                      "b%d%d" % (h, j0), [t_pd[h], t_th])
+        t_b0 = bits(0, 0, 3)
+        t_bp, t_b01, t_b23 = bits(1, 1, 2), bits(1, 0, 1), bits(1, 2, 3)
+        t_pos2 = mm(T.PL[:, 128:160], T.BT[:, 8:16, :], T.pm[:], False, True, "PM", [t_b0, t_bp, t_pm])
+        t_selm = vcopy(sel[:, 64:96], T.PL[:, 128:160], "selm", [t_pos2])
+        mm(T.PH[:, 0:256], T.BT[:, 8:16, :], T.pp[:], False, False, None, t_pp)
         for i in range(4):
-            t_ph = mm(T.PH[:, i:256:4], T.BT[:, i & 2], T.pa[:, :, i & 1], False, i == 3, "PH", [t_b23 if i & 2 else t_b01] + t_pa)
-        t_sc = do("v", lambda: V.tensor_tensor_scan(out=T.SC[:], data0=T.RS[:], data1=T.PH[:, 0:256], initial=0.0, op0=OP.add, op1=OP.max), "SC", [t_ph, t_rs])
-        t_sel = vcopy(sel[:, 0:64], T.SC[:, 3:256:4], "sel", [t_sc])
-        free.update(PD=[t_b23], PH=[t_sc], PM=[t_selm])
+            t_ph = mm(T.PH[:, i:256:4], T.BT[:, 8 * (i & 2):8 * (i & 2) + 8, :], T.pa[:, :, i & 1], False, i == 3, "PH", [t_b23 if i & 2 else t_b01] + t_pa)
+        t_sc = [do("v", lambda: V.tensor_tensor_scan(out=T.SC[:, 128 * k:128 * k + 128], data0=T.RS[:], data1=T.PH[:, 128 * k:128 * k + 128],
+                                                     initial=0.0, op0=OP.add, op1=OP.max), "SC%d" % k, [t_ph, t_rs]) for k in range(2)]
+        t_sel = [vcopy(sel[:, 32 * k:32 * k + 32], T.SC[:, 128 * k + 3:128 * k + 128:4], "sel%d" % k, [t_sc[k]]) for k in range(2)]
+        free.update(PD=[t_b23], PH=[t_sc[1]], PL=[t_selm])
         if raw:
             t_pk = prep_sums(l)
         t_a = {k: scopy(XA[:, k[0]:k[1]], MN[:, 0:2 * A].indirect(sel[:, 64 + k[0] // 16:64 + k[1] // 16]), "xa%d" % k[0], [t_selm]) for k in ((0, H), (H, A))}
@@ -282,9 +286,9 @@ def rank_program(g, core, T, topo):
         for s, j in ON_C:
             a0, a1 = PIECES[j][0:2]
             if s == "B":
-                t_b[j] = tt(XB[:, a0:a1], win.indirect(sel[:, a0 // 16:a1 // 16]), XA[:, a0:a1], OP.min, "xb%d" % j, [t_sel, t_a[(0, H) if a0 < H else (H, A)]])
+                t_b[j] = tt(XB[:, a0:a1], win.indirect(sel[:, a0 // 16:a1 // 16]), XA[:, a0:a1], OP.min, "xb%d" % j, [t_sel[0], t_a[(0, H) if a0 < H else (H, A)]])
             else:
-                t_c[j] = tt(XC[:, a0:a1], win.indirect(sel[:, 32 + a0 // 16:32 + a1 // 16]), XB[:, a0:a1], OP.min, "xc%d" % j, [t_b[j]])
+                t_c[j] = tt(XC[:, a0:a1], win.indirect(sel[:, 32 + a0 // 16:32 + a1 // 16]), XB[:, a0:a1], OP.min, "xc%d" % j, [t_sel[1], t_b[j]])
         if raw:
             take_sums(l, t_pk)
             t_conv.append(scopy(T.W[:, M + A:M + 2 * A], T.WB[:, M + A:M + 2 * A], "conv3", []))
@@ -293,7 +297,9 @@ def rank_program(g, core, T, topo):
         for j, (a0, a1, ld) in enumerate(PIECES):
             P, w = T["P%d" % j], T[("sb%d" if raw else "sf%d") % ld]
             t_p = mm(P[:, 0:a1 - a0], w[:], XC[:, a0:a1], False, True, "sh%d" % j, [t_c[j], t_s[ld] if raw else t_sf[ld]])
-            t_ev.append(tt(out[:, o0 + a0:o0 + a1], P[:, 0:a1 - a0], T.CK[:, b + a0:b + a1], OP.min, "ev%d" % j, [t_p, t_ck[l]]))
+            t_ev.append(tt(out[:, o0 + a0:o0 + a1], P[:, 0:a1 - a0], T.CK[:, b + a0:b + a1], OP.min, "ev%d" % j if l == L else "ev", [t_p, t_ck[l]]))
+        if l < L:
+            t_ev = t_ev[-1:]
         free["P"] = t_ev
         if l == L:
             break

@@ -19,36 +19,43 @@ SCRATCH = {
     "shipi": ("sbuf", [128, 64], I32), "handi": ("sbuf", [128, 64], I32),
     "ship16": ("sbuf", [128, 64], U16), "hand16": ("sbuf", [128, 64], U16),
     "PT": ("sbuf", [128, 768], I32), "cu": ("sbuf", [128, 384], U16),
-    "CF": ("sbuf", [128, 2, 4, 32], F32), "TL": ("sbuf", [128, 4, 2, 16], F32),
-    "SB": ("sbuf", [128, N * SR], BF), "SH1": ("sbuf", [128, N * SA], F32), "SH2": ("sbuf", [128, N * SA], F32),
+    "SB": ("sbuf", [128, N * SR], BF), "SH1": ("sbuf", [128, N * SA], BF), "SH2": ("sbuf", [128, N * SA], F32),
+    "SK": ("sbuf", [128, N * SA], BF), "LK": ("sbuf", [128, N * SA], BF), "LU": ("sbuf", [128, N * SA], BF),
     "BT": ("sbuf", [128, 24, 16], BF), "SC": ("sbuf", [128, 256], F32), "RS": ("sbuf", [128, 128], F32),
     "CP": ("sbuf", [128, L * A], BF), "ST": ("sbuf", [128, L * A], BF), "CK": ("sbuf", [128, L * A], F32),
-    "YB": ("sbuf", [128, A], F32),
-    "xi": ("sbuf", [128, 128], I32), "dist": ("sbuf", [128, 128], I32), "dq": ("sbuf", [128, 96], I32),
-    "dc": ("sbuf", [128, 64, 4], I32), "dcm": ("sbuf", [128, 64, 4], I32), "pos": ("sbuf", [128, 32], I32), "posm": ("sbuf", [128, 32], I32),
+    "SL": ("sbuf", [128, N * SA], F32), "U1": ("sbuf", [128, A], BF), "YB": ("sbuf", [128, A], F32),
+    "xi": ("sbuf", [128, 160], I32), "dist": ("sbuf", [128, 128], I32), "dq": ("sbuf", [128, 96], I32),
+    "dc": ("sbuf", [128, 32, 4], I32), "dcm": ("sbuf", [128, 32, 4], I32), "pos": ("sbuf", [128, 32], I32), "posm": ("sbuf", [128, 32], I32),
     "posf": ("sbuf", [128, 32], F32),
     "sb1": ("sbuf", [128, 8, 16], BF), "sb2": ("sbuf", [128, 8, 16], BF), "sf1": ("sbuf", [128, 128], F32), "sf2": ("sbuf", [128, 128], F32),
-    "idn": ("sbuf", [128, 128], BF), "idf": ("sbuf", [128, 128], F32),
-    "x00": ("sbuf", [128, 128], F32), "x01": ("sbuf", [128, 128], F32), "x10": ("sbuf", [128, 128], F32), "x11": ("sbuf", [128, 128], F32),
-    "qb": ("sbuf", [128, 96], BF), "qf": ("sbuf", [128, 96], F32), "ZR": ("sbuf", [128, 192], BF), "TH": ("sbuf", [128, 192], BF),
-    "CN": ("sbuf", [128, 64, 4], BF), "pp": ("sbuf", [128, 64, 4], BF), "pa": ("sbuf", [128, 64, 2], BF), "pm": ("sbuf", [128, 32], BF),
-    "PD0": ("psum", [128, 64, 8], F32), "PD1": ("psum", [128, 64, 8], F32), "PH": ("psum", [128, 512], F32), "PL": ("psum", [128, 512], F32),
-    "PK": ("psum", [128, 512], F32), "P0": ("psum", [128, 512], F32), "P1": ("psum", [128, 512], F32), "P2": ("psum", [128, 512], F32),
+    "idn": ("sbuf", [128, 128], BF), "idf": ("sbuf", [128, 128], F32), "x0": ("sbuf", [128, 160], F32), "x1": ("sbuf", [128, 160], F32),
+    "qb": ("sbuf", [128, 96], BF), "qf": ("sbuf", [128, 96], F32), "ZR": ("sbuf", [128, 288], BF), "TH": ("sbuf", [128, 288], BF),
+    "CN": ("sbuf", [128, 2, 32, 4], BF), "pp": ("sbuf", [128, 32, 4], BF), "pa": ("sbuf", [128, 2, 32, 2], BF), "pm": ("sbuf", [128, 32], BF),
+    "PD0": ("psum", [128, 32, 16], F32), "PD1": ("psum", [128, 32, 16], F32), "PH0": ("psum", [128, 512], F32), "PH1": ("psum", [128, 512], F32),
+    "P0": ("psum", [128, 512], F32), "P1": ("psum", [128, 512], F32), "P2": ("psum", [128, 512], F32), "P3": ("psum", [128, 512], F32),
 }
 for _l in range(1, L + 1):
     _t = BF if _l == 1 else F32
+    SCRATCH.update({"CF%d" % _l: ("sbuf", [128, 2, 4, 32], F32), "TL%d" % _l: ("sbuf", [128, 4, 2, 16], F32)})
     SCRATCH.update({"G%d" % _l: ("sbuf", [128, 2 * A], _t), "MN%d" % _l: ("sbuf", [128, 2 * A], _t), "sel%d" % _l: ("sbuf", [128, 96], U16),
                     "XA%d" % _l: ("sbuf", [128, A], _t), "XB%d" % _l: ("sbuf", [128, A], _t), "XC%d" % _l: ("sbuf", [128, A], _t)})
-NPOOL = 140
-SEMAPHORES = ["arr0", "arr1", "arr2", "loc0", "loc1", "loc2"] + ["s%d" % i for i in range(NPOOL)]
-PIECES = [(0, 256, 1), (256, 384, 2), (384, 512, 2)]
-ON_A = [("v", "G", 1, 0, 128), ("s", "G", 0, 0, 128), ("s", "G", 0, 128, 256), ("s", "G", 1, 128, 256), ("s", "G", 0, 256, 512), ("s", "G", 1, 256, 384),
-        ("s", "G", 1, 384, 512), ("v", "M", 1, 0, 128), ("v", "M", 0, 0, 128), ("v", "M", 0, 128, 256), ("v", "M", 1, 128, 256), ("v", "M", 0, 256, 512),
-        ("v", "M", 1, 256, 384), ("v", "M", 1, 384, 512)]
-ON_C = [("B", 0), ("B", 1), ("C", 0), ("B", 2), ("C", 1), ("C", 2)]
-BLOCKS = [("G", 1, 0), ("G", 0, 0), ("G", 0, 1), ("M", 1, 0), ("M", 0, 0), ("G", 1, 1), ("M", 0, 1), ("G", 0, 2), ("M", 1, 1),
-          ("G", 0, 3), ("G", 1, 2), ("G", 1, 3), ("M", 0, 2), ("M", 0, 3), ("M", 1, 2), ("M", 1, 3)]
+NPOOL = 130
+SEMAPHORES = ["arr0", "arr1", "arr2", "arrk", "loc0", "loc1", "loc2", "lock"] + ["from%d" % i for i in range(N)] + ["s%d" % i for i in range(NPOOL)]
 DIFFS = {("G", 0): (0, 8, 64, 96), ("M", 0): (0, 16, 32, 96), ("G", 1): (16, 24, 64, 96), ("M", 1): (8, 24, 0, 64)}
+BANK = [0, 0, 0, 1]
+ON_A = [("G", "v", 512, 640), ("G", "s", 0, 256), ("M", "v", 512, 640), ("G", "s", 256, 384), ("M", "v", 0, 128), ("G", "s", 640, 896),
+        ("M", "v", 128, 384), ("G", "s", 384, 512), ("M", "v", 640, 896), ("G", "s", 896, 1024), ("M", "v", 384, 512), ("M", "v", 896, 1024)]
+BLOCKS = [("G", 4), ("G", 1), ("G", 0), ("G", 2), ("M", 4), ("M", 0), ("G", 5), ("G", 6), ("M", 1), ("G", 3), ("M", 2), ("M", 5), ("M", 6),
+          ("M", 3), ("G", 7), ("M", 7)]
+ON_C = {
+    1: [("XA", "s", 0, 256), ("XA", "s", 256, 512), ("XB", "v", 0, 256), ("shift", 0, "B", 0, 256), ("XC", "s", 0, 256), ("XB", "v", 256, 512),
+        ("shift", 2, "B", 256, 512), ("XC", "s", 256, 512), ("out", 0), ("shift", 1, "C", 0, 256), ("shift", 3, "C", 256, 512), ("out", 2), ("out", 1), ("out", 3)],
+    2: [("XA", "s", 0, 192), ("XA", "s", 192, 320), ("XB", "v", 0, 192), ("XA", "s", 320, 512), ("shift", 0, "B", 0, 192), ("XB", "v", 192, 320),
+        ("XC", "s", 0, 192), ("XB", "v", 320, 512), ("XC", "v", 192, 320), ("shift", 1, "C", 0, 192), ("shift", 2, "C", 192, 320), ("XC", "v", 320, 512),
+        ("out", 0), ("out", 2), ("out", 1), ("shift", 3, "C", 320, 512), ("out", 3)],
+}
+ON_C[3] = ON_C[2]
+STORES = [("y", 0, 320), ("s", 320, 512)]
 
 
 def rank_program(g, core, T, topo):
@@ -102,6 +109,11 @@ def rank_program(g, core, T, topo):
     def scopy(out, a, role, deps):
         return do("s", lambda: S.activation(out=out, in_=a, func=AF.Copy), role, deps)
 
+    def scale(out, a, c, role, deps):
+        return do("s", lambda: S.activation(out=out, in_=a, func=AF.Copy, scale=c), role, deps)
+
+    copy = {"v": vcopy, "s": scopy}
+
     def mm(out, w, m, start, stop, role, deps):
         return do("t", lambda: PE.matmul(out=out, lhsT=w, rhs=m, start=start, stop=stop), role, deps)
 
@@ -110,6 +122,9 @@ def rank_program(g, core, T, topo):
 
     def iota(out, pat, base, cm, role, **kw):
         return do("g", lambda: g.iota(out, pat, base, cm, **kw), role, [])
+
+    def widen(out, a, n, role, deps):
+        return do("g", lambda: g.affine_select(out, a, [[0, n]], OP.is_ge, 0.0, 0, 0), role, deps)
 
     here = topo.cores_of(core)
     far = [r for r in range(N) if topo.host(T.cores[r]) != topo.host(core)]
@@ -123,119 +138,152 @@ def rank_program(g, core, T, topo):
     calls = [[r] for r in order]
     calls[1] = calls[1] + buddy
     share = {r: off for r in order}
-    for j, r in enumerate(buddy):
-        share[r] = rest[4 * j:4 * j + 4:2]
+    for r in buddy:
+        share[r] = rest[0::2]
     landed = sum(len(v) for v in share.values())
 
-    def send(ranks, src, dst, w_src, w_dst, k, deps):
+    def send(ranks, src, dst, per, w_dst, engines, there, left, deps):
         for d in deps:
             wait("g", d)
         tr = []
         for r in ranks:
             rid, pid = topo.addr(T.cores[r], core)
-            tr.append(RemoteDMATransfer(src=src[:, r * w_src:(r + 1) * w_src], dst=dst[:, w_dst + rank * w_src:w_dst + (rank + 1) * w_src],
-                                        dst_ids=[DstId(rid=rid, pnc=pid)], dma_engine_mask=sum(1 << e for e in share[r]),
-                                        remote_sem=T.sem["arr%d" % k]))
-        g.remote_dma_fused(tr, local_sem=T.sem["loc%d" % k])
+            tr.append(RemoteDMATransfer(src=src[:, r * per:(r + 1) * per], dst=dst[:, w_dst + rank * per:w_dst + (rank + 1) * per],
+                                        dst_ids=[DstId(rid=rid, pnc=pid)], dma_engine_mask=sum(1 << e for e in engines[r]), remote_sem=T.sem[there]))
+        g.remote_dma_fused(tr, local_sem=T.sem[left])
 
-    def hand_over(win, lists, col0, per, stage, dst, w_dst, k, deps):
+    def hand_over(win, lists, col0, per, stage, dst, w_dst, there, left, deps, calls=calls):
         per16 = per // 16
 
-        def pick(copy, b, e, tag):
-            return copy(stage[:, 16 * b:16 * e], win.indirect(lists[:, col0 + b:col0 + e]), "hand%d" % tag, deps)
+        def pick(q, b, e, tag):
+            return copy[q](stage[:, 16 * b:16 * e], win.indirect(lists[:, col0 + b:col0 + e]), "hand%d" % tag, deps)
         for j, grp in enumerate(calls):
             if j == 0:
                 b = grp[0] * per16
-                pick(vcopy, b, b + per16 // 2, j)
-                t = pick(scopy, b + per16 // 2, b + per16, j)
+                pick("v", b, b + per16 // 2, j)
+                t = pick("s", b + per16 // 2, b + per16, j)
             else:
                 for i, r in enumerate(grp):
-                    t = pick((scopy, vcopy)[(i + j) % 2], r * per16, (r + 1) * per16, j)
-            send(grp, stage, dst, per, w_dst, k, [t])
+                    t = pick("sv"[(i + j) % 2], r * per16, (r + 1) * per16, j)
+            send(grp, stage, dst, per, w_dst, share, there, left, [t])
+
+    def own_slots(win, lists, col0, per, dst, w_dst, deps):
+        per16 = per // 16
         return scopy(dst[:, w_dst + rank * per:w_dst + (rank + 1) * per], win.indirect(lists[:, col0 + rank * per16:col0 + (rank + 1) * per16]), "handown", deps)
 
-    t_sup = dma("y", T.WB[:, 0:M], T.sup[:], "sup")
     t_ship = dma("s", T.shipi[:], T.ship[:], "ship")
-    t_pt = {1: dma("s", T.PT[:, 0:256], T.parts[:, 0:256], "pt1")}
-    t_hand = dma("s", T.handi[:], T.hand[:], "hand")
+    dma("y", T.WB[0:64, 0:M], T.sup[0:64, :], "sup")
+    t_sup = dma("s", T.WB[64:128, 0:M], T.sup[64:128, :], "sup")
+    t_pt = {1: dma("y", T.PT[:, 0:256], T.parts[:, 0:256], "pt1")}
+    t_hand = dma("y", T.handi[:], T.hand[:], "hand")
+    t_st = {1: dma("y", T.ST[:, 0:A], T.stock[:, 0:A], "st1")}
+    t_pt[2] = dma("y", T.PT[:, 256:512], T.parts[:, 256:512], "pt2")
+    t_cp = {1: dma("y", T.CP[:, 0:A], T.cap[:, 0:A], "cp1")}
 
-    t_xi = iota(T.xi[:], [[-32, 4], [1000, 2], [-1, 16]], 0, 1, "xi")
+    small = {"allow_small_or_imprecise_dtypes": True}
+    t_xi = iota(T.xi[:], [[-32, 5], [984, 2], [-1, 16]], 16, 1, "xi")
     t_dq = iota(T.dq[:], [[0, 3], [-16, 8], [0, 4]], -15, 1, "dq")
     t_dist = iota(T.dist[:], [[1, 128]], 0, -1, "dist")
-    t_dc = iota(T.dc[:], [[0, 2], [-1, 32], [0, 4]], 128, 1, "dc")
+    t_dc = iota(T.dc[:], [[-1, 32], [0, 4]], 128, 1, "dc")
     t_pos = iota(T.pos[:], [[1, 32]], 0, 32, "pos")
-    t_cn = [iota(T.CN[:, 0:32, :], [[0, 32], [-int(PEN), 2], [int(PEN), 2]], -int(PEN), 0, "cn0", allow_small_or_imprecise_dtypes=True),
-            iota(T.CN[:, 32:64, :], [[0, 32], [-int(PEN), 2], [-int(PEN), 2]], 0, 0, "cn1", allow_small_or_imprecise_dtypes=True)]
-    t_rs = fill(T.RS[:, 0:128:4], -1048576.0, "rs", [fill(T.RS[:], 0.0, "rs0")])
-    t_zr = fill(T.ZR[:], 0.0, "zr")
+    t_rs0 = fill(T.RS[:], 0.0, "rs0")
     t_th0 = fill(T.TH[:], HUGE, "th0")
-    t_x = [ts(T["x%d%d" % (hb, e)][:], T.xi[:], 16 * hb + 1000 * e, OP.is_equal, "x%d%d" % (hb, e), [t_xi]) for hb in range(2) for e in range(2)]
-    X = [[T.x00, T.x01], [T.x10, T.x11]]
+    t_zr = fill(T.ZR[:], 0.0, "zr")
+    t_rs = fill(T.RS[:, 0:128:4], -1048576.0, "rs", [t_rs0])
     for j in range(4):
-        t_th = fill(T.TH[32 * j:32 * j + 32, j:192:4], 0.0, "th", [t_th0])
+        t_th = fill(T.TH[32 * j:32 * j + 32, j:288:4], 0.0, "th", [t_th0])
+    t_x = [ts(T["x%d" % hb][:], T.xi[:], 1000 * (1 - hb), OP.is_equal, "x%d" % hb, [t_xi]) for hb in range(2)]
+    X = [[T.x0[:, 16:144], T.x0[:, 0:128]], [T.x1[:, 32:160], T.x1[:, 16:144]]]
     t_qb = [where(T.qb[:, 0:64], T.dq[:, 0:64], 0, -1.0, "qb0", [t_dq]), where(T.qb[:, 64:96], T.dq[:, 64:96], 0, 1.0, "qb1", [t_dq])]
     t_idn = ts(T.idn[:], T.dist[:], 0, OP.is_equal, "idn", [t_dist])
     t_dcm = ts(T.dcm[:], T.dc[:], 31, OP.bitwise_and, "dcm", [t_dc])
-    t_idf = scopy(T.idf[:], T.idn[:], "idf", [t_idn])
-    t_qf = [scopy(T.qf[:], T.qb[:], "qf", t_qb)]
-
     t_ship16 = vcopy(T.ship16[:], T.shipi[:], "ship16", [t_ship])
-    t_own = hand_over(T.WB[:, 0:M], T.ship16, 0, SR, T.SB, T.WB, M, 0, [t_ship16, t_sup])
+    t_idf = scopy(T.idf[:], T.idn[:], "idf", [t_idn])
+
+    hand_over(T.WB[:, 0:M], T.ship16, 0, SR, T.SB, T.WB, M, "arr0", "loc0", [t_ship16, t_sup])
+    t_own = own_slots(T.WB[:, 0:M], T.ship16, 0, SR, T.WB, M, [t_ship16, t_sup])
+    t_cn = [iota(T.CN[:, 0], [[0, 32], [int(PEN), 2], [-int(PEN), 2]], -int(PEN), 0, "cn0", **small),
+            iota(T.CN[:, 1], [[0, 32], [-int(PEN), 2], [-int(PEN), 2]], 0, 0, "cn1", **small)]
+    t_conv = [widen(T.W[:, 0:M // 2], T.WB[:, 0:M // 2], M // 2, "conv0", [t_sup])]
 
     wait("y", ("loc0", landed))
-    t_cs = {1: [dma("y", T.CP[:, 0:A], T.cap[:, 0:A], "cp1"), dma("y", T.ST[:, 0:A], T.stock[:, 0:A], "st1")]}
-    t_pt[2] = t_pt[3] = dma("y", T.PT[:, 256:768], T.parts[:, 256:768], "pt2")
-    t_cs[2] = t_cs[3] = [dma("y", T.CP[:, A:3 * A], T.cap[:, A:3 * A], "cp2"), dma("y", T.ST[:, A:3 * A], T.stock[:, A:3 * A], "st2")]
+    t_cp[2] = t_cp[3] = dma("y", T.CP[:, A:3 * A], T.cap[:, A:3 * A], "cp2")
+    t_st[2] = t_st[3] = dma("y", T.ST[:, A:3 * A], T.stock[:, A:3 * A], "st2")
+    t_pt[3] = dma("y", T.PT[:, 512:768], T.parts[:, 512:768], "pt3")
 
-    t_cu, t_pre, t_ck = {}, {}, {}
-    free = {"PD": [], "PH": [], "PM": [], "PL": [], "PK": [], "P": [], "CF": []}
+    t_cf, t_tl, t_pl, t_cu, t_ck = {}, {}, {}, {}, {1: t_cp[1]}
+    free = {k: [] for k in ("PD0", "PD1", "PH0", "PH1", "P0", "P1", "P2", "P3")}
+    wide = [4 * BANK.count(h) for h in range(2)]
 
-    def prep_lists(l, more):
-        b, c = (l - 1) * 256, (l - 1) * 128
-        t_cf = vcopy(T.CF[:], T.PT[:, b:b + 256], "CF", [t_pt[l]] + free["CF"])
-        t_tl = do("v", lambda: V.transpose(out=T.TL[:], in_=T.CF[:, 0]), "TL", [t_cf])
+    def numbers(l):
+        t_cf[l] = vcopy(T["CF%d" % l][:], T.PT[:, (l - 1) * 256:l * 256], "CF%d" % l, [t_pt[l]])
+
+    def turn(l):
+        t_tl[l] = do("v", lambda: V.transpose(out=T["TL%d" % l][:], in_=T["CF%d" % l][:, 0]), "TL%d" % l, [t_cf[l]])
+
+    def swap(l, PL):
         for hb in range(2):
             for e in range(2):
-                t_pl = mm(T.PL[:, hb:128:2], X[hb][e][:], T.TL[:, :, e, :], e == 0, e == 1, "PL", t_x + [t_tl] + free["PL"])
-        t_posf = more()
-        t_cu[l] = vcopy(T.cu[:, c:c + 128], T.PL[:, 0:128], "cu", [t_pl])
-        for PD in (T.PD0, T.PD1):
-            mm(PD[:, 0:24, :], T.idn[:], T.ZR[:], True, False, None, [t_idn, t_zr] + free["PD"])
-        mm(T.PH[:, 0:256], T.idn[:], T.CN[:], True, False, None, t_cn + free["PH"])
-        for i in range(4):
-            t = mm(T.PH[:, i:256:4], T.idf[:], T.CF[:, :, i, :], False, False, "pre", [t_idf])
-        free["CF"] = [t]
-        mm(T.PL[:, 128:160], T.idf[:], T.posf[:], True, False, None, [t_posf, t_cu[l]])
+                t_pl[l] = mm(T[PL][:, hb:128:2], X[hb][e], T["TL%d" % l][:, :, e, :], e == 0, e == 1, "PL%d" % l, t_x + [t_tl[l]] + free[PL])
 
-    def prep_sums(l):
-        b = (l - 1) * A
-        for j, (a0, a1, ld) in enumerate(PIECES):
-            mm(T["P%d" % j][:, 0:a1 - a0], T.idn[:], T.ST[:, b + a0:b + a1], True, False, None, t_cs[l] + free["P"])
-        mm(T.PK[:], T.idn[:], T.CP[:, b:b + A], True, False, None, free["PK"])
-        return mm(T.PK[:], T.idn[:], T.ST[:, b:b + A], False, True, "PK", [])
+    def lists(l, PL):
+        t_cu[l] = vcopy(T.cu[:, (l - 1) * 128:l * 128], T[PL][:, 0:128], "cu%d" % l, [t_pl[l]])
+        free[PL] = [t_cu[l]]
+
+    def sums(l):
+        s = (l - 1) * A
+        mm(T.PD1[:], T.idn[:], T.CP[:, s:s + A], True, False, None, [t_cp[l]] + free["PD1"])
+        return mm(T.PD1[:], T.idn[:], T.ST[:, s:s + A], False, True, "PK", [t_st[l]])
 
     def take_sums(l, t):
-        t_ck[l] = scopy(T.CK[:, (l - 1) * A:l * A], T.PK[:], "CK", [t])
-        free["PK"] = [t_ck[l]]
+        t_ck[l] = scopy(T.CK[:, (l - 1) * A:l * A], T.PD1[:], "CK", [t])
+        free["PD1"] = [t_ck[l]]
 
-    got = {}
+    def answers(l):
+        for k in range(2):
+            PH = T["PH%d" % k]
+            mm(PH[:, 0:128], T.idn[:], T.CN[:, k], True, False, None, [t_idn] + t_cn + free["PH%d" % k])
+            for i in range(4):
+                mm(PH[:, 2 * (i % 2) + i // 2:128:4], T.idf[:], T["CF%d" % l][:, k, i, :], False, False, None, [t_idf, t_cf[l]])
+        for h in (0, 1):
+            mm(T["PD%d" % h][:, 0:24, 0:wide[h]], T.idn[:], T.ZR[:, 0:24 * wide[h]], True, False, None, [t_zr] + free["PD%d" % h])
 
-    def more_constants():
-        t = ts(T.posm[:], T.pos[:], 511, OP.bitwise_and, "posm", [t_pos])
-        got["pp"] = [where(T.pp[:, :, 0:2], T.dcm[:, :, 0:2], 0, -PEN, "pp0", [t_dcm]), where(T.pp[:, :, 2:4], T.dcm[:, :, 2:4], 0, PEN, "pp1", [t_dcm])]
-        got["posf"] = ts(T.posf[:], T.posm[:], float(A), OP.add, "posf", [t])
-        return got["posf"]
-    prep_lists(1, more_constants)
-    t_pp = got["pp"]
-    t_pa = [ts(T.pa[:, 0:32, :], T.pp[:, 0:32, 1:3], -1.0, OP.mult, "pa0", t_pp), vcopy(T.pa[:, 32:64, :], T.pp[:, 0:32, 1:3], "pa1", t_pp)]
-    t_pm = ts(T.pm[:], T.pp[:, 0:32, 0], A / PEN, OP.mult, "pm", t_pp)
+    def stock(l):
+        s = (l - 1) * A
+        for st in ON_C[l]:
+            if st[0] == "shift":
+                mm(T["P%d" % st[1]][:, 0:st[4] - st[3]], T.idn[:], T.ST[:, s + st[3]:s + st[4]], True, False, None, free["P%d" % st[1]])
+
+    numbers(1)
+    t_hand16 = vcopy(T.hand16[:], T.handi[:], "hand16", [t_hand])
+    turn(1)
+    swap(1, "P0")
+    numbers(2)
+    t_pp = [where(T.pp[:, :, 0:4:2], T.dcm[:, :, 0:2], 0, -PEN, "pp0", [t_dcm]), where(T.pp[:, :, 1:4:2], T.dcm[:, :, 2:4], 0, PEN, "pp1", [t_dcm])]
+    turn(2)
+    swap(2, "P1")
+    lists(1, "P0")
     t_s, t_sf = {}, {}
     for ld in (1, 2):
         t_s[ld] = ts(T["sb%d" % ld][:], T.dist[:], ld, OP.is_equal, "sa%d" % ld, [t_dist])
-    t_hand16 = vcopy(T.hand16[:], T.handi[:], "hand16", [t_hand])
+    t_posm = ts(T.posm[:], T.pos[:], 511, OP.bitwise_and, "posm", [t_pos])
     for ld in (1, 2):
         t_s[ld] = fill(T["sb%d" % ld][:, :, 0:ld], 0.0, "sb%d" % ld, [t_s[ld]])
-    t_conv = [scopy(T.W[:, 0:M // 2], T.WB[:, 0:M // 2], "conv0", []), scopy(T.W[:, M // 2:M], T.WB[:, M // 2:M], "conv1", [])]
+    t_posf = ts(T.posf[:], T.posm[:], float(A), OP.add, "posf", [t_posm])
+    lists(2, "P1")
+    answers(1)
+    t_sk = scopy(T.SK[:], T.ST[:, 0:A].indirect(T.hand16[:, 0:32]), "sk", [t_hand16, t_st[1]])
+    t_pa = [scale(T.pa[:, 0], T.pp[:, :, 0:2], -1.0, "pa0", t_pp), scopy(T.pa[:, 1], T.pp[:, :, 0:2], "pa1", t_pp)]
+    t_pm = scale(T.pm[:], T.pp[:, :, 0], A / PEN, "pm", t_pp)
+    early, whole = order[:-1], order[-1:] + buddy
+    send(early, T.SK, T.LK, SA, 0, {r: [e] for r, e in zip(early, off)}, "arrk", "lock", [t_sk])
+    t_conv.append(widen(T.W[:, M:M + 2 * A], T.WB[:, M:M + 2 * A], 2 * A, "conv2", [t_own, ("arr0", landed)]))
+    for ld in (1, 2):
+        t_sf[ld] = widen(T["sf%d" % ld][:], T["sb%d" % ld][:], 128, "sf%d" % ld, [t_s[ld]])
+    t_qf = [widen(T.qf[:], T.qb[:], 96, "qf", t_qb)]
+
+    def over(done, a0, a1):
+        return [t for (b0, b1), t in done.items() if b0 < a1 and a0 < b1]
 
     ready = [t_own, t_sup, ("arr0", landed)]
     for l in range(1, L + 1):
@@ -243,79 +291,108 @@ def rank_program(g, core, T, topo):
         win = (T.WB if raw else T.W)[:, 0:first(l)]
         G, MN, sel, XA, XB, XC = (T["%s%d" % (n, l)] for n in ("G", "MN", "sel", "XA", "XB", "XC"))
         c, b = (l - 1) * 128, (l - 1) * A
-        t_a = {}
-        for qu, kind, p, a0, a1 in ON_A:
-            o = c + (2 * p + (kind == "M")) * 32
-            part = win.indirect(T.cu[:, o + a0 // 16:o + a1 // 16])
-            role, dep = "%s%d_%d" % (kind, p, a0), [t_cu[l]] + ready
+        done = {k: {} for k in ("G", "M", "XA", "XB", "XC", "out")}
+        for kind, qu, a0, a1 in ON_A:
+            o = c + 32 * (a0 // A + (kind == "M"))
+            part, role, dep = win.indirect(T.cu[:, o + a0 // 16:o + a1 // 16]), "%s%d" % (kind, a0), [t_cu[l]] + ready
             if kind == "G":
-                t = (vcopy if qu == "v" else scopy)(G[:, p * A + a0:p * A + a1], part, role, dep)
+                done[kind][a0, a1] = copy[qu](G[:, a0:a1], part, role, dep)
             else:
-                t = tt(MN[:, p * A + a0:p * A + a1], part, G[:, p * A + a0:p * A + a1], OP.min, role,
-                       dep + [t_a[k] for k in t_a if k[0:2] == ("G", p) and k[2] < a1 and a0 < k[3]])
-            t_a[(kind, p, a0, a1)] = t
+                done[kind][a0, a1] = tt(MN[:, a0:a1], part, G[:, a0:a1], OP.min, role, dep + over(done["G"], a0, a1))
+        if raw:
+            t_conv.append(scopy(T.W[:, M // 2:M], T.WB[:, M // 2:M], "conv1", []))
         q, t_q = (T.qb, t_qb) if raw else (T.qf, t_qf)
         t_pd = {}
-        for n, (kind, p, y) in enumerate(BLOCKS):
-            src = G if kind == "G" else MN
-            r0, r1, q0, q1 = DIFFS[(kind, p)]
-            t_pd[y // 2] = mm(T["PD%d" % (y // 2)][:, r0:r1, 4 * (y % 2):4 * (y % 2) + 4], src[:, p * A + 128 * y:p * A + 128 * y + 128], q[:, q0:q1],
-                              False, all(z // 2 != y // 2 for _, _, z in BLOCKS[n + 1:]), "PD%d" % (y // 2),
-                              [t_a[k] for k in t_a if k[0:2] == (kind, p) and k[2] <= 128 * y < k[3]] + t_q)
-        if raw:
-            t_conv.append(scopy(T.W[:, M:M + A], T.WB[:, M:M + A], "conv2", []))
-
-        def bits(h, j0, j1):
-            return tt(T.BT[:, 8 * j0:8 * j1, 8 * h:8 * h + 8], T["PD%d" % h][:, 8 * j0:8 * j1, :], T.TH[:, 0:64 * (j1 - j0)], OP.is_gt,
-                      "b%d%d" % (h, j0), [t_pd[h], t_th])
-        t_b0 = bits(0, 0, 3)
-        t_bp, t_b01, t_b23 = bits(1, 1, 2), bits(1, 0, 1), bits(1, 2, 3)
-        t_pos2 = mm(T.PL[:, 128:160], T.BT[:, 8:16, :], T.pm[:], False, True, "PM", [t_b0, t_bp, t_pm])
-        t_selm = vcopy(sel[:, 64:96], T.PL[:, 128:160], "selm", [t_pos2])
-        mm(T.PH[:, 0:256], T.BT[:, 8:16, :], T.pp[:], False, False, None, t_pp)
-        for i in range(4):
-            t_ph = mm(T.PH[:, i:256:4], T.BT[:, 8 * (i & 2):8 * (i & 2) + 8, :], T.pa[:, :, i & 1], False, i == 3, "PH", [t_b23 if i & 2 else t_b01] + t_pa)
-        t_sc = [do("v", lambda: V.tensor_tensor_scan(out=T.SC[:, 128 * k:128 * k + 128], data0=T.RS[:], data1=T.PH[:, 128 * k:128 * k + 128],
-                                                     initial=0.0, op0=OP.add, op1=OP.max), "SC%d" % k, [t_ph, t_rs]) for k in range(2)]
+        for n, (kind, z) in enumerate(BLOCKS):
+            r0, r1, q0, q1 = DIFFS[kind, z // 4]
+            h = BANK[z % 4]
+            y = 4 * (z % 4 - BANK.index(h))
+            t_pd[h] = mm(T["PD%d" % h][:, r0:r1, y:y + 4], (G if kind == "G" else MN)[:, 128 * z:128 * z + 128], q[:, q0:q1],
+                         False, all(BANK[z2 % 4] != h for _, z2 in BLOCKS[n + 1:]), "PD%d" % h, over(done[kind], 128 * z, 128 * z + 128) + t_q)
+        t_b = [tt(T.BT[:, :, 4 * BANK.index(h):4 * BANK.index(h) + wide[h]], T["PD%d" % h][:, 0:24, 0:wide[h]], T.TH[:, 0:24 * wide[h]], OP.is_gt,
+                  "b%d" % h, [t_pd[h], t_th]) for h in range(2)]
+        mm(T.PD0[:, 30:32, :], T.idf[:], T.posf[:], True, False, None, [t_posf, t_b[0]])
+        t_pos2 = mm(T.PD0[:, 30:32, :], T.BT[:, 8:16, :], T.pm[:], False, True, "PM", t_b + [t_pm])
+        t_ph = []
+        for k in range(2):
+            PH = T["PH%d" % k]
+            mm(PH[:, 0:128], T.BT[:, 8:16, :], T.pp[:], False, False, None, t_pp)
+            mm(PH[:, 0:128:2], T.BT[:, 0:8, :], T.pa[:, k], False, False, None, t_pa)
+            t_ph.append(mm(PH[:, 1:128:2], T.BT[:, 16:24, :], T.pa[:, k], False, True, "PH%d" % k, []))
+        if not raw:
+            stock(l)
+        t_selm = vcopy(sel[:, 64:96], T.PD0[:, 30:32, :], "selm", [t_pos2])
+        t_sc = [do("v", lambda: V.tensor_tensor_scan(out=T.SC[:, 128 * k:128 * k + 128], data0=T.RS[:], data1=T["PH%d" % k][:, 0:128],
+                                                     initial=0.0, op0=OP.add, op1=OP.max), "SC%d" % k, [t_ph[k], t_rs]) for k in range(2)]
         t_sel = [vcopy(sel[:, 32 * k:32 * k + 32], T.SC[:, 128 * k + 3:128 * k + 128:4], "sel%d" % k, [t_sc[k]]) for k in range(2)]
-        free.update(PD=[t_b23], PH=[t_sc[1]], PL=[t_selm])
-        if raw:
-            t_pk = prep_sums(l)
-        t_a = {k: scopy(XA[:, k[0]:k[1]], MN[:, 0:2 * A].indirect(sel[:, 64 + k[0] // 16:64 + k[1] // 16]), "xa%d" % k[0], [t_selm]) for k in ((0, H), (H, A))}
-        t_b, t_c = {}, {}
-        for s, j in ON_C:
-            a0, a1 = PIECES[j][0:2]
-            if s == "B":
-                t_b[j] = tt(XB[:, a0:a1], win.indirect(sel[:, a0 // 16:a1 // 16]), XA[:, a0:a1], OP.min, "xb%d" % j, [t_sel[0], t_a[(0, H) if a0 < H else (H, A)]])
+        free.update(PD0=[t_selm], PD1=[t_b[1]], PH0=[t_sc[0]], PH1=[t_sc[1]])
+        out, o0 = {1: (T.U1, 0), 2: (T.W, first(l)), 3: (T.YB, 0)}[l]
+        piece = {}
+        for st in ON_C[l]:
+            k = st[0]
+            if k == "shift":
+                j, tab, a0, a1 = st[1:5]
+                cuts = [a0] + [H] * (a0 < H < a1) + [a1]
+                for x0, x1 in zip(cuts, cuts[1:]):
+                    ld = 1 + x0 // H
+                    t_p = mm(T["P%d" % j][:, x0 - a0:x1 - a0], T[("sb%d" if raw else "sf%d") % ld][:], (XB if tab == "B" else XC)[:, x0:x1], raw, x1 == a1,
+                             "sh%d" % j, over(done["X" + tab], x0, x1) + [t_s[ld] if raw else t_sf[ld]])
+                piece[j] = (a0, a1, t_p)
+            elif k == "out":
+                j = st[1]
+                a0, a1, t_p = piece[j]
+                to, dep = out[:, o0 + a0:o0 + a1], over(done["out"], a0, a1)
+                done[k][a0, a1] = tt(to, T["P%d" % j][:, 0:a1 - a0], to if dep else (T.CP if raw else T.CK)[:, b + a0:b + a1], OP.min, "ev%d" % j, [t_p, t_ck[l]] + dep)
             else:
-                t_c[j] = tt(XC[:, a0:a1], win.indirect(sel[:, 32 + a0 // 16:32 + a1 // 16]), XB[:, a0:a1], OP.min, "xc%d" % j, [t_sel[1], t_b[j]])
-        if raw:
-            take_sums(l, t_pk)
-            t_conv.append(scopy(T.W[:, M + A:M + 2 * A], T.WB[:, M + A:M + 2 * A], "conv3", []))
-        out, o0 = (T.YB, 0) if l == L else (T.W, first(l))
-        t_ev = []
-        for j, (a0, a1, ld) in enumerate(PIECES):
-            P, w = T["P%d" % j], T[("sb%d" if raw else "sf%d") % ld]
-            t_p = mm(P[:, 0:a1 - a0], w[:], XC[:, a0:a1], False, True, "sh%d" % j, [t_c[j], t_s[ld] if raw else t_sf[ld]])
-            t_ev.append(tt(out[:, o0 + a0:o0 + a1], P[:, 0:a1 - a0], T.CK[:, b + a0:b + a1], OP.min, "ev%d" % j if l == L else "ev", [t_p, t_ck[l]]))
-        if l < L:
-            t_ev = t_ev[-1:]
-        free["P"] = t_ev
+                qu, a0, a1 = st[1:4]
+                o, role = {"XA": 64, "XB": 0, "XC": 32}[k], "%s%d" % (k, a0)
+                lst = sel[:, o + a0 // 16:o + a1 // 16]
+                if k == "XA":
+                    done[k][a0, a1] = copy[qu](XA[:, a0:a1], MN[:, 0:2 * A].indirect(lst), role, [t_selm])
+                elif k == "XB":
+                    done[k][a0, a1] = tt(XB[:, a0:a1], win.indirect(lst), XA[:, a0:a1], OP.min, role, [t_sel[0]] + over(done["XA"], a0, a1))
+                elif qu == "v":
+                    done[k][a0, a1] = tt(XC[:, a0:a1], win.indirect(lst), XB[:, a0:a1], OP.min, role, [t_sel[1]] + over(done["XB"], a0, a1))
+                else:
+                    done[k][a0, a1] = scopy(XC[:, a0:a1], win.indirect(lst), role, [t_sel[1]])
+        t_ev = list(done["out"].values())
+        free.update(P0=t_ev, P1=t_ev, P2=t_ev, P3=t_ev)
         if l == L:
             break
         B = first(l)
-        t_own = hand_over(T.W[:, B:B + A], T.hand16, (l - 1) * 32, SA, T["SH%d" % l], T.W, B + A, l, t_ev + [t_hand16])
-        t_pk = prep_sums(l + 1)
-        prep_lists(l + 1, lambda: got["posf"])
+        t_pk = sums(l + 1)
         if raw:
-            for ld in (1, 2):
-                t_sf[ld] = scopy(T["sf%d" % ld][:], T["sb%d" % ld][:], "sf%d" % ld, [t_s[ld]])
-        take_sums(l + 1, t_pk)
-        ready = t_ev + t_conv + [t_own, ("arr%d" % l, landed)]
-    for j, (a0, a1, ld) in enumerate(PIECES):
-        dma("ysy"[j], T.y[:, a0:a1], T.YB[:, a0:a1], "y%d" % j, [t_ev[j]])
+            def summed(to, o, r, role):
+                return tt(to[:, o + r * SA:o + (r + 1) * SA], T.U1[:].indirect(T.hand16[:, 4 * r:4 * r + 4]), T.SK[:, r * SA:(r + 1) * SA], OP.add, role, t_ev + [t_sk])
+            hand_over(T.U1[:], T.hand16, 0, SA, T.SH1, T.LU, 0, "from%d" % rank, "loc1", t_ev, [[r] for r in early])
+            send(whole, T.SL, T.W, SA, B + A, share, "arr1", "loc1", [summed(T.SL, 0, r, "whole") for r in whole][-1:])
+            t_own = summed(T.W, B + A, rank, "handown")
+            numbers(3)
+            mm(T.P3[:], T.idn[:], T.U1[:], True, False, None, t_ev)
+            t_ev = free["P3"] = [scopy(T.W[:, B:B + A], T.P3[:], "own", [mm(T.P3[:], T.idn[:], T.ST[:, 0:A], False, True, "sum", [t_st[1]])])]
+            chips = [(min(grp) * SA, (max(grp) + 1) * SA, grp) for grp in (early[0:2], early[2:4], early[4:])]
+            for a0, a1, grp in chips:
+                t_k = mm(T.P2[:, a0:a1], T.idn[:], T.LK[:, a0:a1], True, True, "lk", [("arrk", len(early))])
+            turn(3)
+            take_sums(l + 1, t_pk)
+            answers(l + 1)
+            for a0, a1, grp in chips:
+                t_add = tt(T.W[:, B + A + a0:B + A + a1], T.P2[:, a0:a1], T.LU[:, a0:a1], OP.add, "add", [t_k] + [("from%d" % r, len(share[r])) for r in grp])
+            free["P2"] = [t_add]
+            ready = t_ev + t_conv + [t_own, t_add, ("arr1", sum(len(share[r]) for r in whole))]
+        else:
+            hand_over(T.W[:, B:B + A], T.hand16, (l - 1) * 32, SA, T.SH2, T.W, B + A, "arr2", "loc2", t_ev)
+            t_own = own_slots(T.W[:, B:B + A], T.hand16, (l - 1) * 32, SA, T.W, B + A, t_ev)
+            swap(l + 1, "P0")
+            lists(l + 1, "P0")
+            take_sums(l + 1, t_pk)
+            answers(l + 1)
+            ready = t_ev + [t_own, ("arr2", landed)]
+    for j, (qu, a0, a1) in enumerate(STORES):
+        dma(qu, T.y[:, a0:a1], T.YB[:, a0:a1], "y%d" % j, over(done["out"], a0, a1))
     for k in range(3):
         wait("g", ("loc%d" % k, landed))
+    wait("g", ("lock", len(early)))
     for name in total:
         if best.get(name, 0) < total[name]:
             wait("g", (name, total[name]))

import numpy as np
from concourse.bass import DstId, RemoteDMATransfer
from concourse.mybir import AluOpType as OP, ActivationFunctionType as AF

M, A, L, SR, SA, N = 2048, 512, 3, 128, 64, 8
H = A // 2
PEN = 8192.0
HUGE = 2.0 ** 80


def first(l):
    return M + N * SR + (l - 1) * (A + N * SA)


BF, F32, I32, U16 = "bfloat16", "float32", "int32", "uint16"
SCRATCH = {
    "WB": ("sbuf", [128, M + N * SR], BF),
    "W": ("sbuf", [128, first(L)], F32),
    "shipi": ("sbuf", [128, 64], I32), "handi": ("sbuf", [128, 64], I32),
    "ship16": ("sbuf", [128, 64], U16), "hand16": ("sbuf", [128, 64], U16),
    "PT": ("sbuf", [128, 768], I32), "cu": ("sbuf", [128, 384], U16),
    "SB": ("sbuf", [128, N * SR], BF), "SH1": ("sbuf", [128, N * SA], BF), "SH2": ("sbuf", [128, N * SA], F32),
    "SK": ("sbuf", [128, N * SA], BF), "LK": ("sbuf", [128, N * SA], BF), "LU": ("sbuf", [128, N * SA], BF),
    "BT": ("sbuf", [128, 24, 16], BF), "SC": ("sbuf", [128, 256], F32), "RS": ("sbuf", [128, 128], F32),
    "CP": ("sbuf", [128, L * A], BF), "ST": ("sbuf", [128, L * A], BF), "CK": ("sbuf", [128, L * A], F32),
    "SL": ("sbuf", [128, N * SA], F32), "U1": ("sbuf", [128, A], BF), "YB": ("sbuf", [128, A], F32),
    "xi": ("sbuf", [128, 160], I32), "dist": ("sbuf", [128, 128], I32), "dq": ("sbuf", [128, 96], I32),
    "dc": ("sbuf", [128, 32, 4], I32), "dcm": ("sbuf", [128, 32, 4], I32), "pos": ("sbuf", [128, 32], I32), "posm": ("sbuf", [128, 32], I32),
    "posf": ("sbuf", [128, 32], F32),
    "sb1": ("sbuf", [128, 8, 16], BF), "sb2": ("sbuf", [128, 8, 16], BF), "sf1": ("sbuf", [128, 128], F32), "sf2": ("sbuf", [128, 128], F32),
    "idn": ("sbuf", [128, 128], BF), "idf": ("sbuf", [128, 128], F32), "x0": ("sbuf", [128, 160], F32), "x1": ("sbuf", [128, 160], F32),
    "qb": ("sbuf", [128, 96], BF), "qf": ("sbuf", [128, 96], F32), "ZR": ("sbuf", [128, 288], BF), "TH": ("sbuf", [128, 288], BF),
    "CN": ("sbuf", [128, 2, 32, 4], BF), "pp": ("sbuf", [128, 32, 4], BF), "pa": ("sbuf", [128, 2, 32, 2], BF), "pm": ("sbuf", [128, 32], BF),
    "PD0": ("psum", [128, 32, 16], F32), "PD1": ("psum", [128, 32, 16], F32), "PH0": ("psum", [128, 512], F32), "PH1": ("psum", [128, 512], F32),
    "P0": ("psum", [128, 512], F32), "P1": ("psum", [128, 512], F32), "P2": ("psum", [128, 512], F32), "P3": ("psum", [128, 512], F32),
}
for _l in range(1, L + 1):
    _t = BF if _l == 1 else F32
    SCRATCH.update({"CF%d" % _l: ("sbuf", [128, 2, 4, 32], F32), "TL%d" % _l: ("sbuf", [128, 4, 2, 16], F32)})
    SCRATCH.update({"G%d" % _l: ("sbuf", [128, 2 * A], _t), "MN%d" % _l: ("sbuf", [128, 2 * A], _t), "sel%d" % _l: ("sbuf", [128, 96], U16),
                    "XA%d" % _l: ("sbuf", [128, A], _t), "XB%d" % _l: ("sbuf", [128, A], _t), "XC%d" % _l: ("sbuf", [128, A], _t)})
NPOOL = 130
SEMAPHORES = ["arr0", "arr1", "arr2", "arrk", "loc0", "loc1", "loc2", "lock"] + ["from%d" % i for i in range(N)] + ["s%d" % i for i in range(NPOOL)]
DIFFS = {("G", 0): (0, 8, 64, 96), ("M", 0): (0, 16, 32, 96), ("G", 1): (16, 24, 64, 96), ("M", 1): (8, 24, 0, 64)}
BANK = [0, 0, 0, 1]
ON_A = [("G", "v", 512, 640), ("G", "s", 0, 256), ("M", "v", 512, 640), ("G", "s", 256, 384), ("M", "v", 0, 128), ("G", "s", 640, 896),
        ("M", "v", 128, 384), ("G", "s", 384, 512), ("M", "v", 640, 896), ("G", "s", 896, 1024), ("M", "v", 384, 512), ("M", "v", 896, 1024)]
BLOCKS = [("G", 4), ("G", 1), ("G", 0), ("G", 2), ("M", 4), ("M", 0), ("G", 5), ("G", 6), ("M", 1), ("G", 3), ("M", 2), ("M", 5), ("M", 6),
          ("M", 3), ("G", 7), ("M", 7)]
ON_C = {
    1: [("XA", "s", 0, 256), ("XA", "s", 256, 512), ("XB", "v", 0, 256), ("shift", 0, "B", 0, 256), ("XC", "s", 0, 256), ("XB", "v", 256, 512),
        ("shift", 2, "B", 256, 512), ("XC", "s", 256, 512), ("out", 0), ("shift", 1, "C", 0, 256), ("shift", 3, "C", 256, 512), ("out", 2), ("out", 1), ("out", 3)],
    2: [("XA", "s", 0, 192), ("XA", "s", 192, 320), ("XB", "v", 0, 192), ("XA", "s", 320, 512), ("shift", 0, "B", 0, 192), ("XB", "v", 192, 320),
        ("XC", "s", 0, 192), ("XB", "v", 320, 512), ("XC", "v", 192, 320), ("shift", 1, "C", 0, 192), ("shift", 2, "C", 192, 320), ("XC", "v", 320, 512),
        ("out", 0), ("out", 2), ("out", 1), ("shift", 3, "C", 320, 512), ("out", 3)],
}
ON_C[3] = ON_C[2]
STORES = [("y", 0, 320), ("s", 320, 512)]


def rank_program(g, core, T, topo):
    rank = T.rank_of(core)
    if rank is None:
        return
    Q = {"v": g.vector, "s": g.scalar, "t": g.tensor, "g": g, "y": g.sync}
    pool, total, seen, best, before = {}, {}, {q: {} for q in Q}, {}, {}

    def wait(q, tok):
        name, val = tok
        if seen[q].get(name, 0) >= val:
            return
        Q[q].wait_ge(T.sem[name], val)
        seen[q][name] = val
        best[name] = max(best.get(name, 0), val)
        for k, v in before.get(tok, {}).items():
            seen[q][k] = max(seen[q].get(k, 0), v)

    def do(q, fn, role, deps, n=1):
        for d in deps:
            wait(q, d)
        inst = fn()
        if role is None:
            return None
        if role not in pool:
            pool[role] = "s%d" % len(pool)
        name = pool[role]
        inst.then_inc(T.sem[name], n)
        total[name] = total.get(name, 0) + n
        before[(name, total[name])] = dict(seen[q])
        return (name, total[name])

    V, S, PE = g.vector, g.scalar, g.tensor

    def tt(out, a, b, op, role, deps):
        return do("v", lambda: V.tensor_tensor(out=out, in0=a, in1=b, op=op), role, deps)

    def ts(out, a, s1, op, role, deps):
        return do("v", lambda: V.tensor_scalar(out=out, in0=a, scalar1=s1, scalar2=None, op0=op), role, deps)

    def where(out, a, v, c, role, deps):
        return do("v", lambda: V.tensor_scalar(out=out, in0=a, scalar1=v, scalar2=c, op0=OP.is_equal, op1=OP.mult), role, deps)

    def fill(out, c, role, deps=()):
        return do("v", lambda: V.memset(out, c), role, deps)

    def vcopy(out, a, role, deps):
        return do("v", lambda: V.tensor_copy(out=out, in_=a), role, deps)

    def scopy(out, a, role, deps):
        return do("s", lambda: S.activation(out=out, in_=a, func=AF.Copy), role, deps)

    def scale(out, a, c, role, deps):
        return do("s", lambda: S.activation(out=out, in_=a, func=AF.Copy, scale=c), role, deps)

    copy = {"v": vcopy, "s": scopy}

    def mm(out, w, m, start, stop, role, deps):
        return do("t", lambda: PE.matmul(out=out, lhsT=w, rhs=m, start=start, stop=stop), role, deps)

    def dma(q, out, in_, role, deps=()):
        return do(q, lambda: Q[q].dma_start(out=out, in_=in_), role, deps, 16)

    def iota(out, pat, base, cm, role, **kw):
        return do("g", lambda: g.iota(out, pat, base, cm, **kw), role, [])

    def widen(out, a, n, role, deps):
        return do("g", lambda: g.affine_select(out, a, [[0, n]], OP.is_ge, 0.0, 0, 0), role, deps)

    here = topo.cores_of(core)
    far = [r for r in range(N) if topo.host(T.cores[r]) != topo.host(core)]
    buddy = [r for r in range(N) if T.cores[r] in here and r != rank]
    near = [r for r in range(N) if r not in far and r not in buddy and r != rank]
    off = topo.engines(core, T.cores[far[0]])
    rest = [e for e in topo.engines(core, T.cores[buddy[0]]) if e not in off]
    plane = [r for r in far if topo.same_plane(core, T.cores[r])]
    farthest = [r for r in far if r not in plane]
    order = [r for grp in (farthest, plane, near) for r in sorted(grp, key=lambda r: topo.die(T.cores[r]) == topo.die(core))]
    calls = [[r] for r in order]
    calls[1] = calls[1] + buddy
    share = {r: off for r in order}
    for r in buddy:
        share[r] = rest[0::2]
    landed = sum(len(v) for v in share.values())

    def send(ranks, src, dst, per, w_dst, engines, there, left, deps):
        for d in deps:
            wait("g", d)
        tr = []
        for r in ranks:
            rid, pid = topo.addr(T.cores[r], core)
            tr.append(RemoteDMATransfer(src=src[:, r * per:(r + 1) * per], dst=dst[:, w_dst + rank * per:w_dst + (rank + 1) * per],
                                        dst_ids=[DstId(rid=rid, pnc=pid)], dma_engine_mask=sum(1 << e for e in engines[r]), remote_sem=T.sem[there]))
        g.remote_dma_fused(tr, local_sem=T.sem[left])

    def hand_over(win, lists, col0, per, stage, dst, w_dst, there, left, deps, calls=calls):
        per16 = per // 16

        def pick(q, b, e, tag):
            return copy[q](stage[:, 16 * b:16 * e], win.indirect(lists[:, col0 + b:col0 + e]), "hand%d" % tag, deps)
        for j, grp in enumerate(calls):
            if j == 0:
                b = grp[0] * per16
                pick("v", b, b + per16 // 2, j)
                t = pick("s", b + per16 // 2, b + per16, j)
            else:
                for i, r in enumerate(grp):
                    t = pick("sv"[(i + j) % 2], r * per16, (r + 1) * per16, j)
            send(grp, stage, dst, per, w_dst, share, there, left, [t])

    def own_slots(win, lists, col0, per, dst, w_dst, deps):
        per16 = per // 16
        return scopy(dst[:, w_dst + rank * per:w_dst + (rank + 1) * per], win.indirect(lists[:, col0 + rank * per16:col0 + (rank + 1) * per16]), "handown", deps)

    t_ship = dma("s", T.shipi[:], T.ship[:], "ship")
    dma("y", T.WB[0:64, 0:M], T.sup[0:64, :], "sup")
    t_sup = dma("s", T.WB[64:128, 0:M], T.sup[64:128, :], "sup")
    t_pt = {1: dma("y", T.PT[:, 0:256], T.parts[:, 0:256], "pt1")}
    t_hand = dma("y", T.handi[:], T.hand[:], "hand")
    t_st = {1: dma("y", T.ST[:, 0:A], T.stock[:, 0:A], "st1")}
    t_pt[2] = dma("y", T.PT[:, 256:512], T.parts[:, 256:512], "pt2")
    t_cp = {1: dma("y", T.CP[:, 0:A], T.cap[:, 0:A], "cp1")}

    small = {"allow_small_or_imprecise_dtypes": True}
    t_xi = iota(T.xi[:], [[-32, 5], [984, 2], [-1, 16]], 16, 1, "xi")
    t_dq = iota(T.dq[:], [[0, 3], [-16, 8], [0, 4]], -15, 1, "dq")
    t_dist = iota(T.dist[:], [[1, 128]], 0, -1, "dist")
    t_dc = iota(T.dc[:], [[-1, 32], [0, 4]], 128, 1, "dc")
    t_pos = iota(T.pos[:], [[1, 32]], 0, 32, "pos")
    t_rs0 = fill(T.RS[:], 0.0, "rs0")
    t_th0 = fill(T.TH[:], HUGE, "th0")
    t_zr = fill(T.ZR[:], 0.0, "zr")
    t_rs = fill(T.RS[:, 0:128:4], -1048576.0, "rs", [t_rs0])
    for j in range(4):
        t_th = fill(T.TH[32 * j:32 * j + 32, j:288:4], 0.0, "th", [t_th0])
    t_x = [ts(T["x%d" % hb][:], T.xi[:], 1000 * (1 - hb), OP.is_equal, "x%d" % hb, [t_xi]) for hb in range(2)]
    X = [[T.x0[:, 16:144], T.x0[:, 0:128]], [T.x1[:, 32:160], T.x1[:, 16:144]]]
    t_qb = [where(T.qb[:, 0:64], T.dq[:, 0:64], 0, -1.0, "qb0", [t_dq]), where(T.qb[:, 64:96], T.dq[:, 64:96], 0, 1.0, "qb1", [t_dq])]
    t_idn = ts(T.idn[:], T.dist[:], 0, OP.is_equal, "idn", [t_dist])
    t_dcm = ts(T.dcm[:], T.dc[:], 31, OP.bitwise_and, "dcm", [t_dc])
    t_ship16 = vcopy(T.ship16[:], T.shipi[:], "ship16", [t_ship])
    t_idf = scopy(T.idf[:], T.idn[:], "idf", [t_idn])

    hand_over(T.WB[:, 0:M], T.ship16, 0, SR, T.SB, T.WB, M, "arr0", "loc0", [t_ship16, t_sup])
    t_own = own_slots(T.WB[:, 0:M], T.ship16, 0, SR, T.WB, M, [t_ship16, t_sup])
    t_cn = [iota(T.CN[:, 0], [[0, 32], [int(PEN), 2], [-int(PEN), 2]], -int(PEN), 0, "cn0", **small),
            iota(T.CN[:, 1], [[0, 32], [-int(PEN), 2], [-int(PEN), 2]], 0, 0, "cn1", **small)]
    t_conv = [widen(T.W[:, 0:M // 2], T.WB[:, 0:M // 2], M // 2, "conv0", [t_sup])]

    wait("y", ("loc0", landed))
    t_cp[2] = t_cp[3] = dma("y", T.CP[:, A:3 * A], T.cap[:, A:3 * A], "cp2")
    t_st[2] = t_st[3] = dma("y", T.ST[:, A:3 * A], T.stock[:, A:3 * A], "st2")
    t_pt[3] = dma("y", T.PT[:, 512:768], T.parts[:, 512:768], "pt3")

    t_cf, t_tl, t_pl, t_cu, t_ck = {}, {}, {}, {}, {1: t_cp[1]}
    free = {k: [] for k in ("PD0", "PD1", "PH0", "PH1", "P0", "P1", "P2", "P3")}
    wide = [4 * BANK.count(h) for h in range(2)]

    def numbers(l):
        t_cf[l] = vcopy(T["CF%d" % l][:], T.PT[:, (l - 1) * 256:l * 256], "CF%d" % l, [t_pt[l]])

    def turn(l):
        t_tl[l] = do("v", lambda: V.transpose(out=T["TL%d" % l][:], in_=T["CF%d" % l][:, 0]), "TL%d" % l, [t_cf[l]])

    def swap(l, PL):
        for hb in range(2):
            for e in range(2):
                t_pl[l] = mm(T[PL][:, hb:128:2], X[hb][e], T["TL%d" % l][:, :, e, :], e == 0, e == 1, "PL%d" % l, t_x + [t_tl[l]] + free[PL])

    def lists(l, PL):
        t_cu[l] = vcopy(T.cu[:, (l - 1) * 128:l * 128], T[PL][:, 0:128], "cu%d" % l, [t_pl[l]])
        free[PL] = [t_cu[l]]

    def sums(l):
        s = (l - 1) * A
        mm(T.PD1[:], T.idn[:], T.CP[:, s:s + A], True, False, None, [t_cp[l]] + free["PD1"])
        return mm(T.PD1[:], T.idn[:], T.ST[:, s:s + A], False, True, "PK", [t_st[l]])

    def take_sums(l, t):
        t_ck[l] = scopy(T.CK[:, (l - 1) * A:l * A], T.PD1[:], "CK", [t])
        free["PD1"] = [t_ck[l]]

    def answers(l):
        for k in range(2):
            PH = T["PH%d" % k]
            mm(PH[:, 0:128], T.idn[:], T.CN[:, k], True, False, None, [t_idn] + t_cn + free["PH%d" % k])
            for i in range(4):
                mm(PH[:, 2 * (i % 2) + i // 2:128:4], T.idf[:], T["CF%d" % l][:, k, i, :], False, False, None, [t_idf, t_cf[l]])
        for h in (0, 1):
            mm(T["PD%d" % h][:, 0:24, 0:wide[h]], T.idn[:], T.ZR[:, 0:24 * wide[h]], True, False, None, [t_zr] + free["PD%d" % h])

    def stock(l):
        s = (l - 1) * A
        for st in ON_C[l]:
            if st[0] == "shift":
                mm(T["P%d" % st[1]][:, 0:st[4] - st[3]], T.idn[:], T.ST[:, s + st[3]:s + st[4]], True, False, None, free["P%d" % st[1]])

    numbers(1)
    t_hand16 = vcopy(T.hand16[:], T.handi[:], "hand16", [t_hand])
    turn(1)
    swap(1, "P0")
    numbers(2)
    t_pp = [where(T.pp[:, :, 0:4:2], T.dcm[:, :, 0:2], 0, -PEN, "pp0", [t_dcm]), where(T.pp[:, :, 1:4:2], T.dcm[:, :, 2:4], 0, PEN, "pp1", [t_dcm])]
    turn(2)
    swap(2, "P1")
    lists(1, "P0")
    t_s, t_sf = {}, {}
    for ld in (1, 2):
        t_s[ld] = ts(T["sb%d" % ld][:], T.dist[:], ld, OP.is_equal, "sa%d" % ld, [t_dist])
    t_posm = ts(T.posm[:], T.pos[:], 511, OP.bitwise_and, "posm", [t_pos])
    for ld in (1, 2):
        t_s[ld] = fill(T["sb%d" % ld][:, :, 0:ld], 0.0, "sb%d" % ld, [t_s[ld]])
    t_posf = ts(T.posf[:], T.posm[:], float(A), OP.add, "posf", [t_posm])
    lists(2, "P1")
    answers(1)
    t_sk = scopy(T.SK[:], T.ST[:, 0:A].indirect(T.hand16[:, 0:32]), "sk", [t_hand16, t_st[1]])
    t_pa = [scale(T.pa[:, 0], T.pp[:, :, 0:2], -1.0, "pa0", t_pp), scopy(T.pa[:, 1], T.pp[:, :, 0:2], "pa1", t_pp)]
    t_pm = scale(T.pm[:], T.pp[:, :, 0], A / PEN, "pm", t_pp)
    early, whole = order[:-1], order[-1:] + buddy
    send(early, T.SK, T.LK, SA, 0, {r: [e] for r, e in zip(early, off)}, "arrk", "lock", [t_sk])
    t_conv.append(widen(T.W[:, M:M + 2 * A], T.WB[:, M:M + 2 * A], 2 * A, "conv2", [t_own, ("arr0", landed)]))
    for ld in (1, 2):
        t_sf[ld] = widen(T["sf%d" % ld][:], T["sb%d" % ld][:], 128, "sf%d" % ld, [t_s[ld]])
    t_qf = [widen(T.qf[:], T.qb[:], 96, "qf", t_qb)]

    def over(done, a0, a1):
        return [t for (b0, b1), t in done.items() if b0 < a1 and a0 < b1]

    ready = [t_own, t_sup, ("arr0", landed)]
    for l in range(1, L + 1):
        raw = l == 1
        win = (T.WB if raw else T.W)[:, 0:first(l)]
        G, MN, sel, XA, XB, XC = (T["%s%d" % (n, l)] for n in ("G", "MN", "sel", "XA", "XB", "XC"))
        c, b = (l - 1) * 128, (l - 1) * A
        done = {k: {} for k in ("G", "M", "XA", "XB", "XC", "out")}
        for kind, qu, a0, a1 in ON_A:
            o = c + 32 * (a0 // A + (kind == "M"))
            part, role, dep = win.indirect(T.cu[:, o + a0 // 16:o + a1 // 16]), "%s%d" % (kind, a0), [t_cu[l]] + ready
            if kind == "G":
                done[kind][a0, a1] = copy[qu](G[:, a0:a1], part, role, dep)
            else:
                done[kind][a0, a1] = tt(MN[:, a0:a1], part, G[:, a0:a1], OP.min, role, dep + over(done["G"], a0, a1))
        if raw:
            t_conv.append(scopy(T.W[:, M // 2:M], T.WB[:, M // 2:M], "conv1", []))
        q, t_q = (T.qb, t_qb) if raw else (T.qf, t_qf)
        t_pd = {}
        for n, (kind, z) in enumerate(BLOCKS):
            r0, r1, q0, q1 = DIFFS[kind, z // 4]
            h = BANK[z % 4]
            y = 4 * (z % 4 - BANK.index(h))
            t_pd[h] = mm(T["PD%d" % h][:, r0:r1, y:y + 4], (G if kind == "G" else MN)[:, 128 * z:128 * z + 128], q[:, q0:q1],
                         False, all(BANK[z2 % 4] != h for _, z2 in BLOCKS[n + 1:]), "PD%d" % h, over(done[kind], 128 * z, 128 * z + 128) + t_q)
        t_b = [tt(T.BT[:, :, 4 * BANK.index(h):4 * BANK.index(h) + wide[h]], T["PD%d" % h][:, 0:24, 0:wide[h]], T.TH[:, 0:24 * wide[h]], OP.is_gt,
                  "b%d" % h, [t_pd[h], t_th]) for h in range(2)]
        mm(T.PD0[:, 30:32, :], T.idf[:], T.posf[:], True, False, None, [t_posf, t_b[0]])
        t_pos2 = mm(T.PD0[:, 30:32, :], T.BT[:, 8:16, :], T.pm[:], False, True, "PM", t_b + [t_pm])
        t_ph = []
        for k in range(2):
            PH = T["PH%d" % k]
            mm(PH[:, 0:128], T.BT[:, 8:16, :], T.pp[:], False, False, None, t_pp)
            mm(PH[:, 0:128:2], T.BT[:, 0:8, :], T.pa[:, k], False, False, None, t_pa)
            t_ph.append(mm(PH[:, 1:128:2], T.BT[:, 16:24, :], T.pa[:, k], False, True, "PH%d" % k, []))
        if not raw:
            stock(l)
        t_selm = vcopy(sel[:, 64:96], T.PD0[:, 30:32, :], "selm", [t_pos2])
        t_sc = [do("v", lambda: V.tensor_tensor_scan(out=T.SC[:, 128 * k:128 * k + 128], data0=T.RS[:], data1=T["PH%d" % k][:, 0:128],
                                                     initial=0.0, op0=OP.add, op1=OP.max), "SC%d" % k, [t_ph[k], t_rs]) for k in range(2)]
        t_sel = [vcopy(sel[:, 32 * k:32 * k + 32], T.SC[:, 128 * k + 3:128 * k + 128:4], "sel%d" % k, [t_sc[k]]) for k in range(2)]
        free.update(PD0=[t_selm], PD1=[t_b[1]], PH0=[t_sc[0]], PH1=[t_sc[1]])
        out, o0 = {1: (T.U1, 0), 2: (T.W, first(l)), 3: (T.YB, 0)}[l]
        piece = {}
        for st in ON_C[l]:
            k = st[0]
            if k == "shift":
                j, tab, a0, a1 = st[1:5]
                cuts = [a0] + [H] * (a0 < H < a1) + [a1]
                for x0, x1 in zip(cuts, cuts[1:]):
                    ld = 1 + x0 // H
                    t_p = mm(T["P%d" % j][:, x0 - a0:x1 - a0], T[("sb%d" if raw else "sf%d") % ld][:], (XB if tab == "B" else XC)[:, x0:x1], raw, x1 == a1,
                             "sh%d" % j, over(done["X" + tab], x0, x1) + [t_s[ld] if raw else t_sf[ld]])
                piece[j] = (a0, a1, t_p)
            elif k == "out":
                j = st[1]
                a0, a1, t_p = piece[j]
                to, dep = out[:, o0 + a0:o0 + a1], over(done["out"], a0, a1)
                done[k][a0, a1] = tt(to, T["P%d" % j][:, 0:a1 - a0], to if dep else (T.CP if raw else T.CK)[:, b + a0:b + a1], OP.min, "ev%d" % j, [t_p, t_ck[l]] + dep)
            else:
                qu, a0, a1 = st[1:4]
                o, role = {"XA": 64, "XB": 0, "XC": 32}[k], "%s%d" % (k, a0)
                lst = sel[:, o + a0 // 16:o + a1 // 16]
                if k == "XA":
                    done[k][a0, a1] = copy[qu](XA[:, a0:a1], MN[:, 0:2 * A].indirect(lst), role, [t_selm])
                elif k == "XB":
                    done[k][a0, a1] = tt(XB[:, a0:a1], win.indirect(lst), XA[:, a0:a1], OP.min, role, [t_sel[0]] + over(done["XA"], a0, a1))
                elif qu == "v":
                    done[k][a0, a1] = tt(XC[:, a0:a1], win.indirect(lst), XB[:, a0:a1], OP.min, role, [t_sel[1]] + over(done["XB"], a0, a1))
                else:
                    done[k][a0, a1] = scopy(XC[:, a0:a1], win.indirect(lst), role, [t_sel[1]])
        t_ev = list(done["out"].values())
        free.update(P0=t_ev, P1=t_ev, P2=t_ev, P3=t_ev)
        if l == L:
            break
        B = first(l)
        t_pk = sums(l + 1)
        if raw:
            def summed(to, o, r, role):
                return tt(to[:, o + r * SA:o + (r + 1) * SA], T.U1[:].indirect(T.hand16[:, 4 * r:4 * r + 4]), T.SK[:, r * SA:(r + 1) * SA], OP.add, role, t_ev + [t_sk])
            hand_over(T.U1[:], T.hand16, 0, SA, T.SH1, T.LU, 0, "from%d" % rank, "loc1", t_ev, [[r] for r in early])
            send(whole, T.SL, T.W, SA, B + A, share, "arr1", "loc1", [summed(T.SL, 0, r, "whole") for r in whole][-1:])
            t_own = summed(T.W, B + A, rank, "handown")
            numbers(3)
            mm(T.P3[:], T.idn[:], T.U1[:], True, False, None, t_ev)
            t_ev = free["P3"] = [scopy(T.W[:, B:B + A], T.P3[:], "own", [mm(T.P3[:], T.idn[:], T.ST[:, 0:A], False, True, "sum", [t_st[1]])])]
            chips = [(min(grp) * SA, (max(grp) + 1) * SA, grp) for grp in (early[0:2], early[2:4], early[4:])]
            for a0, a1, grp in chips:
                t_k = mm(T.P2[:, a0:a1], T.idn[:], T.LK[:, a0:a1], True, True, "lk", [("arrk", len(early))])
            turn(3)
            take_sums(l + 1, t_pk)
            answers(l + 1)
            for a0, a1, grp in chips:
                t_add = tt(T.W[:, B + A + a0:B + A + a1], T.P2[:, a0:a1], T.LU[:, a0:a1], OP.add, "add", [t_k] + [("from%d" % r, len(share[r])) for r in grp])
            free["P2"] = [t_add]
            ready = t_ev + t_conv + [t_own, t_add, ("arr1", sum(len(share[r]) for r in whole))]
        else:
            hand_over(T.W[:, B:B + A], T.hand16, (l - 1) * 32, SA, T.SH2, T.W, B + A, "arr2", "loc2", t_ev)
            t_own = own_slots(T.W[:, B:B + A], T.hand16, (l - 1) * 32, SA, T.W, B + A, t_ev)
            swap(l + 1, "P0")
            lists(l + 1, "P0")
            take_sums(l + 1, t_pk)
            answers(l + 1)
            ready = t_ev + [t_own, ("arr2", landed)]
    for j, (qu, a0, a1) in enumerate(STORES):
        dma(qu, T.y[:, a0:a1], T.YB[:, a0:a1], "y%d" % j, over(done["out"], a0, a1))
    for k in range(3):
        wait("g", ("loc%d" % k, landed))
    wait("g", ("lock", len(early)))
    for name in total:
        if best.get(name, 0) < total[name]:
            wait("g", (name, total[name]))
